import numpy as np
import ml_dtypes


def mxq(x, axis, fmt="e4m3"):
    dtype, down = {"e4m3": (ml_dtypes.float8_e4m3fn, 7), "e5m2": (ml_dtypes.float8_e5m2, 14)}[fmt]
    v = np.moveaxis(np.asarray(x, np.float32).astype(ml_dtypes.bfloat16).astype(np.float64), axis, -1)
    blocks = v.reshape(v.shape[:-1] + (-1, 32))
    amax = np.abs(blocks).max(-1, keepdims=True)
    byte = np.maximum(np.where(amax > 0, np.frexp(amax)[1] - 1 + 127, 0) - down, 1)
    scale = np.exp2(byte - 127.0)
    codes = (blocks / scale).astype(np.float32).astype(dtype).astype(np.float64)
    return np.moveaxis((codes * scale).reshape(v.shape), -1, axis)


WIDE = False


def mx_kscale(k):
    if not WIDE:
        return np.ones(k)
    levels = np.array([10, -10, 5, -5, 0])
    if k % 512:
        return np.exp2(np.random.permutation(np.resize(levels, k // 32))).repeat(32)
    a = np.empty((k // 512, 16))
    for p in range(k // 512):
        a[p, :8] = np.random.permutation(np.resize(levels, 8))
        for g in range(8):
            far = levels[np.abs(levels - a[p, g]) >= 10]
            a[p, g + 8] = far[np.random.randint(len(far))]
    return np.exp2(a.ravel()).repeat(32)


BF16 = ml_dtypes.bfloat16


def bf(x):
    return np.asarray(x, np.float32).astype(BF16)


def f64(x):
    return np.asarray(x).astype(np.float64)


E2M1 = np.array([0.0, 0.5, 1.0, 1.5, 2.0, 3.0, 4.0, 6.0, -0.0, -0.5, -1.0, -1.5, -2.0, -3.0, -4.0, -6.0])


def pack_weight(w, fmt):
    k, n = w.shape
    w = f64(bf(w)).reshape(k // 32, 32, n)
    amax = np.abs(w).max(1)
    if fmt == "e4m3":
        byte = np.frexp(amax)[1] - 1 + 127 - 7
    else:
        mant, ex = np.frexp(amax / 6.0)
        byte = np.where(mant > 0.5, ex, ex - 1) + 127
    byte = np.clip(np.where(amax > 0, byte, 1), 1, 254)
    scaled = (w * np.exp2(127.0 - byte)[:, None, :]).reshape(k, n).astype(np.float32)
    by_word = np.ascontiguousarray(scaled.reshape(k // 512, 128, 4, n).transpose(0, 1, 3, 2))
    if fmt == "e4m3":
        words = by_word.astype(ml_dtypes.float8_e4m3fn).view(np.uint8)
    else:
        c = by_word.astype(ml_dtypes.float4_e2m1fn).view(np.uint8) & 0xF
        words = c[..., 0::2] | (c[..., 1::2] << 4)
    return np.ascontiguousarray(words), np.ascontiguousarray(byte.astype(np.uint8).reshape(k // 512, 16, n))


def unpack_weight(words, scales, fmt):
    g, p, n, _ = words.shape
    if fmt == "e4m3":
        vals = np.ascontiguousarray(words).view(ml_dtypes.float8_e4m3fn).astype(np.float64)
    else:
        nib = np.empty((g, p, n, 4), np.uint8)
        nib[..., 0::2] = words & 0xF
        nib[..., 1::2] = words >> 4
        vals = E2M1[nib]
    vals = vals * np.repeat(np.exp2(scales.astype(np.float64) - 127.0), 8, axis=1)[..., None]
    return vals.transpose(0, 1, 3, 2).reshape(g * 512, n)
def pack4(w):
    words, scales = pack_weight(w, "e2m1")
    return words.reshape(words.shape[0], 128, -1), scales


def unpack4(words, scales):
    return unpack_weight(words.reshape(words.shape[0], 128, -1, 2), scales, "e2m1")


B, HI, W, C, ND, P, O = 2, 4, 512, 1024, 512, 1024, 512


def softmax_last(t):
    e = np.exp(t - np.max(t, axis=-1, keepdims=True))
    return e / np.sum(e, axis=-1, keepdims=True)


def prime_context(x, wc_words, wc_scales, gw):
    y = mxq(f64(x), 3, "e4m3") @ unpack4(wc_words, wc_scales)
    m = np.max(y, axis=1)
    centred = m - np.mean(m, axis=-1, keepdims=True)
    return centred * f64(gw)[None, :, None]


def prime_depth(dl, gd):
    n_depth = dl.shape[-1]
    return (n_depth * softmax_last(f64(dl))) * f64(gd)[None, None, :]


def draw0():
    s = mx_kscale(C)
    t = mx_kscale(ND)
    u = mx_kscale(W)
    x = bf(np.random.standard_normal((B, HI, W, C)) * s)
    wc_words, wc_scales = pack4(np.random.standard_normal((C, O)) / np.sqrt(C) / s[:, None])
    gw = bf((1.0 + 0.1 * np.random.standard_normal(W)) / u)
    dl = bf(1.5 * np.random.standard_normal((B, W, ND)))
    gd = bf(np.random.standard_normal(ND) * t)
    ring_words, ring_scales = pack4((np.random.standard_normal((P, ND)) / np.sqrt(ND) / t[None, :]).T)
    ray = bf(np.random.standard_normal((P, W)) / np.sqrt(W) * u[None, :])
    return {
        "x": x,
        "wc_words": wc_words,
        "wc_scales": wc_scales,
        "gw": gw,
        "dl": dl,
        "gd": gd,
        "ring_words": ring_words,
        "ring_scales": ring_scales,
        "ray": ray,
    }


def core(x, wc_words, wc_scales, gw, dl, gd, ring_words, ring_scales, ray):
    ctx = prime_context(x, wc_words, wc_scales, gw)
    d = prime_depth(dl, gd)
    rd = unpack4(ring_words, ring_scales).T @ mxq(d, 2, "e4m3").transpose(0, 2, 1)
    tm = rd * f64(ray)[None, :, :]
    return mxq(tm, 2, "e4m3") @ mxq(ctx, 1, "e4m3")


def e4m3fn_bytes(y):
    return np.clip(np.asarray(y, np.float64), -448.0, 448.0).astype(np.float32).astype(ml_dtypes.float8_e4m3fn).view(np.uint8)


def e4m3fn_values(b):
    return np.asarray(b, np.uint8).view(ml_dtypes.float8_e4m3fn).astype(np.float64)


def setup_inputs():
    d = draw0()
    x0 = np.asarray(d['x']).astype(np.float64)
    s = (np.max(np.abs(x0), axis=(0, 1, 2), keepdims=True) / 448.0).astype(np.float32)
    out = {}
    for k, v in d.items():
        if k == 'x':
            out['x_bytes'] = e4m3fn_bytes(x0 / s.astype(np.float64))
            out['x_scale'] = s
        else:
            out[k] = v
    return out


def reference(x_bytes, x_scale, wc_words, wc_scales, gw, dl, gd, ring_words, ring_scales, ray):
    return core(e4m3fn_values(x_bytes) * x_scale.astype(np.float64), wc_words, wc_scales, gw, dl, gd, ring_words, ring_scales, ray)

@@ -1,0 +1,433 @@
+from contextlib import ExitStack
+
+import concourse.mybir as mybir
+from concourse.masks import make_identity
+
+F32 = mybir.dt.float32
+BF16 = mybir.dt.bfloat16
+I32 = mybir.dt.int32
+U32 = mybir.dt.uint32
+U8 = mybir.dt.uint8
+F8 = mybir.dt.float8_e4m3fn
+FP8X4 = mybir.dt.float8_e4m3fn_x4
+FP4X4 = mybir.dt.float4_e2m1fn_x4
+ALU = mybir.AluOpType
+ACT = mybir.ActivationFunctionType
+AXIS = mybir.AxisListType
+
+B, HI, W, C, ND, CELLS, O = 2, 4, 512, 1024, 512, 1024, 512
+P = 128
+T = 4
+G = C // 512
+NC = CELLS // P
+FLOPS = 2 * B * HI * W * C * O + 2 * B * CELLS * W * ND + 2 * B * CELLS * W * O
+
+
+def tile_matrixvtringraybev_w4_kernel(tc, x_bytes, x_scale, wc_words, wc_scales, gw, dl, gd, ring_words, ring_scales, ray, out):
+    nc = tc.nc
+    with ExitStack() as ctx:
+        keep = ctx.enter_context(tc.tile_pool(name="keep", bufs=1))
+        per_b = ctx.enter_context(tc.tile_pool(name="per_b", bufs=2))
+        raws = ctx.enter_context(tc.tile_pool(name="raws", bufs=8))
+        flow = ctx.enter_context(tc.tile_pool(name="flow", bufs=3))
+        stores = ctx.enter_context(tc.tile_pool(name="stores", bufs=8))
+        ps_t = ctx.enter_context(tc.psum_pool(name="ps_t", bufs=3))
+        ps_y = ctx.enter_context(tc.psum_pool(name="ps_y", bufs=5))
+        ctx.enter_context(tc.manual_schedule())
+
+        warm = keep.tile([P, 1], F32, name="warm")
+        nc.vector.memset(warm[:], 0.0)
+        warm_out = keep.tile([P, 1], F32, name="warm_out")
+        nc.scalar.activation(out=warm_out[:], in_=warm[:], func=ACT.Exp)
+
+        ident = keep.tile([P, P], F32, name="ident", align_bytes=64)
+        make_identity(nc, ident[:])
+        w_planes = keep.tile([P, G * O + CELLS], U8, name="w_planes", align_bytes=64)
+        nc.gpsimd.memset(w_planes[:].bitcast(I32), 0)
+
+        sc8 = keep.tile([P, 8], F32, name="sc8")
+        nc.scalar.dma_start(out=sc8[:], in_=x_scale.rearrange("a b c (p j) -> p (a b c j)", p=P))
+        gd4 = keep.tile([P, 4], BF16, name="gd4")
+        nc.scalar.dma_start(out=gd4[:], in_=gd.rearrange("(p j) -> p j", p=P))
+        gw4 = keep.tile([P, 4], BF16, name="gw4")
+        nc.scalar.dma_start(out=gw4[:], in_=gw.rearrange("(p j) -> p j", p=P))
+
+        dls = []
+        raw = []
+        for b in range(B):
+            dl_b = per_b.tile([P, T, ND], BF16, name="dl_b", align_bytes=64)
+            dls.append(dl_b)
+        for i in range(B * HI):
+            raw_i = raws.tile([P, T, C], U8, name="raw_i", align_bytes=64)
+            raw.append(raw_i)
+        wc = keep.tile([P, G, 2 * O], U8, name="wc", align_bytes=64)
+        ring = keep.tile([P, 2 * CELLS], U8, name="ring", align_bytes=64)
+        ray_raw = keep.tile([P, NC, W], BF16, name="ray_raw", align_bytes=64)
+
+        def load_dl(b):
+            nc.sync.dma_start(out=dls[b][:], in_=dl[b].rearrange("(p t) n -> p t n", t=T))
+
+        def load_x(i, t0, t1):
+            src = x_bytes[i // HI, i % HI].rearrange("(p t) c -> p t c", t=T)
+            nc.sync.dma_start(out=raw[i][:, t0:t1, :], in_=src[:, t0:t1, :])
+
+        load_dl(0)
+        load_x(0, 0, 1)
+        load_x(0, 1, 4)
+        for q in range(4):
+            rows = slice(32 * q, 32 * q + 4)
+            nc.sync.dma_start(
+                out=w_planes[rows, 0 : G * O].bitcast(I32).rearrange("q (g n) -> q g n", g=G),
+                in_=wc_scales[:, 4 * q : 4 * q + 4, :].bitcast(I32).rearrange("g q n -> q g n"),
+            )
+        for q in range(4):
+            rows = slice(32 * q, 32 * q + 4)
+            nc.sync.dma_start(
+                out=w_planes[rows, G * O :].bitcast(I32),
+                in_=ring_scales[0, 4 * q : 4 * q + 4, :].bitcast(I32),
+            )
+        nc.sync.dma_start(out=wc[:].bitcast(I32), in_=wc_words.bitcast(I32).rearrange("g p n -> p g n"))
+        load_x(1, 0, 4)
+        nc.sync.dma_start(out=ray_raw[:], in_=ray.rearrange("(c p) w -> p c w", p=P))
+        nc.sync.dma_start(out=ring[:].bitcast(I32), in_=ring_words[0].bitcast(I32))
+        load_dl(1)
+        for i in range(2, B * HI):
+            load_x(i, 0, 4)
+
+        scale = keep.tile([P, C], F32, name="scale", align_bytes=64)
+        gd512 = keep.tile([P, ND], F32, name="gd512", align_bytes=64)
+        gd4f = keep.tile([P, 4], F32, name="gd4f")
+        gwf = keep.tile([P, 4], F32, name="gwf")
+        gwn = keep.tile([P, 4], F32, name="gwn")
+
+        def spread_scale(j):
+            xt = ps_t.tile([P, 4, P], F32, name="xt")
+            for c in range(4):
+                col = 4 * j + c
+                nc.tensor.transpose(xt[:, c, :], sc8[:, col : col + 1].to_broadcast([P, P]), ident[:])
+            nc.scalar.copy(
+                out=scale[:].rearrange("p (n c) -> p n c", c=8)[:, :, 4 * j : 4 * j + 4],
+                in_=xt[:].rearrange("p c n -> p n c"),
+            )
+
+        def small_vectors():
+            nc.vector.tensor_scalar(out=gd4f[:], in0=gd4[:], scalar1=float(ND), scalar2=None, op0=ALU.mult)
+            nc.vector.tensor_copy(out=gwf[:], in_=gw4[:])
+            nc.vector.tensor_scalar(out=gwn[:], in0=gw4[:], scalar1=-1.0 / O, scalar2=None, op0=ALU.mult)
+
+        def spread_gd():
+            xt = ps_t.tile([P, 4, P], F32, name="xt")
+            for c in range(4):
+                nc.tensor.transpose(xt[:, c, :], gd4f[:, c : c + 1].to_broadcast([P, P]), ident[:])
+            nc.scalar.copy(out=gd512[:].rearrange("p (n c) -> p n c", c=4), in_=xt[:].rearrange("p c n -> p n c"))
+
+        negmax, esum, rsum, e_t, d_t, dg, d_codes, d_planes = {}, {}, {}, {}, {}, {}, {}, {}
+        tmg, tm_codes, tm_planes = {}, {}, {}
+        ray_t = keep.tile([P, NC, P, T], BF16, name="ray_t", align_bytes=64)
+
+        m1, m2, mx = {}, {}, {}
+
+        def d_max_step(b, k):
+            if k == 0:
+                m1[b] = per_b.tile([P, T, ND // 2], BF16, name="m1_b")
+                m2[b] = per_b.tile([P, T, ND // 4], BF16, name="m2_b")
+                mx[b] = per_b.tile([P, T], F32, name="mx_b")
+                negmax[b] = per_b.tile([P, T], F32, name="negmax_b")
+                esum[b] = per_b.tile([P, T], F32, name="esum_b")
+                nc.vector.tensor_max(out=m1[b][:], in0=dls[b][:, :, 0 : ND // 2], in1=dls[b][:, :, ND // 2 :])
+            elif k == 1:
+                nc.vector.tensor_max(out=m2[b][:], in0=m1[b][:, :, 0 : ND // 4], in1=m1[b][:, :, ND // 4 :])
+            elif k == 2:
+                nc.vector.reduce_max(out=mx[b][:], in_=m2[b][:], axis=AXIS.X)
+            else:
+                nc.vector.tensor_scalar(out=negmax[b][:], in0=mx[b][:], scalar1=-1.0, scalar2=None, op0=ALU.mult)
+                d_tiles(b)
+
+        def d_tiles(b):
+            e_t[b] = per_b.tile([P, T, ND], F32, name="e_b", align_bytes=64)
+            d_t[b] = per_b.tile([P, T, ND], BF16, name="d_b", align_bytes=64)
+            dg[b] = per_b.tile([P, T, P, T], BF16, name="dg_b", align_bytes=64)
+            d_codes[b] = per_b.tile([P, W], U32, name="dcodes_b", align_bytes=64)
+            d_planes[b] = per_b.tile([P, W], U8, name="dplanes_b", align_bytes=64)
+            tm_codes[b] = per_b.tile([P, CELLS], U32, name="tmcodes_b", align_bytes=64)
+            tm_planes[b] = per_b.tile([P, CELLS], U8, name="tmplanes_b", align_bytes=64)
+
+        def d_exp(b, t):
+            nc.scalar.activation(
+                out=e_t[b][:, t, :], in_=dls[b][:, t, :], func=ACT.Exp, bias=negmax[b][:, t : t + 1], accum_out=esum[b][:, t : t + 1]
+            )
+
+        def d_recip(b):
+            rsum[b] = per_b.tile([P, T], F32, name="rsum_b")
+            nc.vector.reciprocal(out=rsum[b][:], in_=esum[b][:])
+
+        def d_mul(b, t):
+            nc.vector.scalar_tensor_tensor(
+                out=d_t[b][:, t, :], in0=e_t[b][:, t, :], scalar=rsum[b][:, t : t + 1], in1=gd512[:], op0=ALU.mult, op1=ALU.mult
+            )
+
+        turned = {}
+
+        def turn_pair(key, words, first):
+            xt = ps_t.tile([P, 2, 2, P], F32, name="xt")
+            for j in range(2):
+                for u in range(2):
+                    start = 256 * (first + j)
+                    nc.tensor.transpose(xt[:, j, u, :], words[:, start + u : start + 256 : 2], ident[:])
+            turned[key] = xt
+
+        def untangle(key, dst):
+            nc.scalar.copy(
+                out=dst.rearrange("p j n k -> p (j n k)").bitcast(F32).rearrange("p (j n u) -> p j n u", j=2, u=2),
+                in_=turned[key][:].rearrange("p j u n -> p j n u"),
+            )
+
+        def d_turn(b, h):
+            turn_pair(("d", b, h), d_t[b][:].rearrange("p t n -> p (t n)").bitcast(F32), 2 * h)
+
+        def d_copy(b, h):
+            untangle(("d", b, h), dg[b][:, 2 * h : 2 * h + 2, :, :])
+
+        def d_quant(b):
+            nc.vector.quantize_mx(
+                out=d_codes[b][:].bitcast(FP8X4), scales=d_planes[b][:], in_=dg[b][:].rearrange("p t w k -> p (t w k)")
+            )
+
+        def ray_turn(i):
+            turn_pair(("ray", i), ray_raw[:].rearrange("p c w -> p (c w)").bitcast(F32), 2 * i)
+
+        def ray_copy(i):
+            untangle(("ray", i), ray_t[:, 2 * i : 2 * i + 2, :, :])
+
+        rds = {}
+
+        def transport(b, c):
+            rd = ps_y.tile([P, T, P], F32, name="acc")
+            for t in range(T):
+                nc.tensor.matmul_mx(
+                    out=rd[:, t, :],
+                    lhsT=d_codes[b][:, P * t : P * (t + 1)].bitcast(FP8X4),
+                    lhsT_scale=d_planes[b][:, P * t : P * (t + 1)],
+                    rhs=ring[:, 2 * P * c : 2 * P * (c + 1)].bitcast(FP4X4),
+                    rhs_scale=w_planes[:, G * O + P * c : G * O + P * (c + 1)],
+                    start=True,
+                    stop=True,
+                )
+            rds[b, c] = rd
+
+        def weigh(b, c):
+            rd = rds[b, c]
+            if c % 4 == 0:
+                tmg[b, c // 4] = per_b.tile([P, 4, P, T], BF16, name="tmg_b", align_bytes=64)
+            nc.vector.tensor_tensor(
+                out=tmg[b, c // 4][:, c % 4, :, :], in0=rd[:].rearrange("p t n -> p n t"), in1=ray_t[:, c, :, :], op=ALU.mult
+            )
+
+        def tm_quant(b, h):
+            nc.vector.quantize_mx(
+                out=tm_codes[b][:, 512 * h : 512 * (h + 1)].bitcast(FP8X4),
+                scales=tm_planes[b][:, 512 * h : 512 * (h + 1)],
+                in_=tmg[b, h][:].rearrange("p c n k -> p (c n k)"),
+            )
+
+        n_units = B * HI * T
+        xs, xg, x_codes, x_planes, y_ps, m_t, msum, ctxg, c_codes, c_planes = {}, {}, {}, {}, {}, {}, {}, {}, {}, {}
+
+        def scale_rows(q):
+            i, t = divmod(q, T)
+            xs[q] = flow.tile([P, C], BF16, name="xs_q", align_bytes=64)
+            nc.vector.tensor_tensor(out=xs[q][:], in0=raw[i][:, t, :].bitcast(F8), in1=scale[:], op=ALU.mult)
+
+        def turn(q):
+            pair, k = divmod(q, 2)
+            if k == 0:
+                xg[pair] = flow.tile([P, 2, G, P, T], BF16, name="xg_p", align_bytes=64)
+                x_codes[pair] = flow.tile([P, 2, G, P], U32, name="xcodes_p", align_bytes=64)
+                x_planes[pair] = flow.tile([P, 2, G, P], U8, name="xplanes_p", align_bytes=64)
+            xt = ps_t.tile([P, G, 2, P], F32, name="xt")
+            words = xs[q][:].bitcast(F32)
+            for g in range(G):
+                for u in range(2):
+                    nc.tensor.transpose(xt[:, g, u, :], words[:, 256 * g + u : 256 * (g + 1) : 2], ident[:])
+            nc.scalar.copy(
+                out=xg[pair][:, k].rearrange("p g r k -> p (g r k)").bitcast(F32).rearrange("p (g r u) -> p g r u", g=G, u=2),
+                in_=xt[:].rearrange("p g u r -> p g r u"),
+            )
+
+        def quant(pair, k0, k1):
+            nc.vector.quantize_mx(
+                out=x_codes[pair][:, k0:k1].rearrange("p k g r -> p (k g r)").bitcast(FP8X4),
+                scales=x_planes[pair][:, k0:k1].rearrange("p k g r -> p (k g r)"),
+                in_=xg[pair][:, k0:k1].rearrange("p k g r j -> p (k g r j)"),
+            )
+
+        def project(q):
+            pair, k = divmod(q, 2)
+            y_ps[q] = ps_y.tile([P, O], F32, name="acc")
+            for g in range(G):
+                nc.tensor.matmul_mx(
+                    out=y_ps[q][:],
+                    lhsT=x_codes[pair][:, k, g, :].bitcast(FP8X4),
+                    lhsT_scale=x_planes[pair][:, k, g, :],
+                    rhs=wc[:, g, :].bitcast(FP4X4),
+                    rhs_scale=w_planes[:, O * g : O * (g + 1)],
+                    start=(g == 0),
+                    stop=(g == G - 1),
+                )
+
+        def height_max(q):
+            i, t = divmod(q, T)
+            b, h = divmod(i, HI)
+            if h == 0 and t == 0:
+                m_t[b] = per_b.tile([P, T, O], F32, name="m_b", align_bytes=64)
+                msum[b] = per_b.tile([P, T], F32, name="msum_b")
+                ctxg[b] = per_b.tile([P, O, T], BF16, name="ctxg_b", align_bytes=64)
+                c_codes[b] = per_b.tile([P, O], U32, name="ccodes_b", align_bytes=64)
+                c_planes[b] = per_b.tile([P, O], U8, name="cplanes_b", align_bytes=64)
+            m = m_t[b][:, t, :]
+            if h == 0:
+                nc.scalar.copy(out=m, in_=y_ps[q][:])
+            elif h < HI - 1:
+                nc.vector.tensor_max(out=m, in0=y_ps[q][:], in1=m)
+            else:
+                nc.vector.scalar_tensor_tensor(
+                    out=m, in0=y_ps[q][:], scalar=1.0, in1=m, op0=ALU.mult, op1=ALU.max, accum_out=msum[b][:, t : t + 1]
+                )
+
+        def centre(b, t):
+            bias = per_b.tile([P, 1], F32, name="bias")
+            nc.scalar.activation(out=bias[:], in_=msum[b][:, t : t + 1], func=ACT.Copy, scale=gwn[:, t : t + 1])
+            nc.scalar.activation(
+                out=ctxg[b][:, :, t], in_=m_t[b][:, t, :], func=ACT.Identity, scale=gwf[:, t : t + 1], bias=bias[:]
+            )
+
+        def ctx_quant(b):
+            nc.vector.quantize_mx(
+                out=c_codes[b][:].bitcast(FP8X4), scales=c_planes[b][:], in_=ctxg[b][:].rearrange("p o t -> p (o t)")
+            )
+
+        accs = {}
+
+        def result(b, c):
+            acc = ps_y.tile([P, O], F32, name="acc")
+            nc.tensor.matmul_mx(
+                out=acc[:],
+                lhsT=tm_codes[b][:, P * c : P * (c + 1)].bitcast(FP8X4),
+                lhsT_scale=tm_planes[b][:, P * c : P * (c + 1)],
+                rhs=c_codes[b][:].bitcast(FP8X4),
+                rhs_scale=c_planes[b][:],
+                start=True,
+                stop=True,
+            )
+            accs[b, c] = acc
+
+        def emit(b, c, on_vector):
+            acc = accs[b, c]
+            res = stores.tile([P, O], F32, name="res", align_bytes=64)
+            if on_vector:
+                nc.vector.tensor_copy(out=res[:], in_=acc[:])
+            else:
+                nc.scalar.copy(out=res[:], in_=acc[:])
+            nc.sync.dma_start(out=out[b, P * c : P * (c + 1), :], in_=res[:])
+
+        pe, act, vec = {}, {}, {}
+
+        def at(table, q, fn, *args):
+            table.setdefault(q, []).append((fn, args))
+
+        def run(table, q):
+            for fn, args in table.get(q, []):
+                fn(*args)
+
+        at(vec, 1, d_recip, 0)
+        for t in range(T):
+            at(vec, 2 + t // 2, d_mul, 0, t)
+        for h in range(2):
+            at(pe, 3 + h, d_turn, 0, h)
+            at(act, 4 + h, d_copy, 0, h)
+        at(vec, 7, d_quant, 0)
+        for i in range(4):
+            at(pe, 5 + i, ray_turn, i)
+            at(act, 6 + i, ray_copy, i)
+        for c in range(NC):
+            at(pe, 8 + c, transport, 0, c)
+            at(vec, 10 + c, weigh, 0, c)
+        at(vec, 14, tm_quant, 0, 0)
+        at(vec, 18, tm_quant, 0, 1)
+        for k in range(4):
+            at(vec, 4 + k, d_max_step, 1, k)
+        for t in range(T):
+            at(act, 10 + t, d_exp, 1, t)
+        at(vec, 15, d_recip, 1)
+        for t in range(T):
+            at(vec, 16 + t, d_mul, 1, t)
+        for h in range(2):
+            at(pe, 19 + 2 * h, d_turn, 1, h)
+            at(act, 20 + 2 * h, d_copy, 1, h)
+        at(vec, 23, d_quant, 1)
+        for t in range(T):
+            at(act, 19 + t, centre, 0, t)
+        at(vec, 24, ctx_quant, 0)
+        for c in range(NC - 1):
+            at(pe, 25 + c, result, 0, c)
+            at(act, 26 + c, emit, 0, c, False)
+        for c in range(3):
+            at(pe, 25 + 2 * c, transport, 1, c)
+            at(vec, 27 + 2 * c, weigh, 1, c)
+
+        for k in range(4):
+            d_max_step(0, k)
+        small_vectors()
+        for j in range(2):
+            spread_scale(j)
+        for t in range(T):
+            d_exp(0, t)
+        spread_gd()
+        for q in range(n_units):
+            if q >= 4:
+                project(q - 4)
+            run(pe, q)
+            run(act, q)
+            run(vec, q)
+            if q >= 6:
+                height_max(q - 6)
+            scale_rows(q)
+            turn(q)
+            if q >= 3 and q % 2 == 1:
+                quant((q - 3) // 2, 0, 2)
+        last = n_units - 1
+        project(last - 3)
+        emit(0, NC - 2, False)
+        height_max(last - 5)
+        quant(last // 2, 0, 1)
+        project(last - 2)
+        height_max(last - 4)
+        result(0, NC - 1)
+        project(last - 1)
+        height_max(last - 3)
+        emit(0, NC - 1, False)
+        centre(1, 0)
+        transport(1, 3)
+        quant(last // 2, 1, 2)
+        project(last)
+        height_max(last - 2)
+        centre(1, 1)
+        transport(1, 4)
+        weigh(1, 3)
+        height_max(last - 1)
+        centre(1, 2)
+        transport(1, 5)
+        tm_quant(1, 0)
+        height_max(last)
+        centre(1, 3)
+        weigh(1, 4)
+        transport(1, 6)
+        weigh(1, 5)
+        transport(1, 7)
+        weigh(1, 6)
+        weigh(1, 7)
+        ctx_quant(1)
+        tm_quant(1, 1)
+        for c in range(NC):
+            result(1, c)
+            emit(1, c, c % 2 == 1)

@@ -20,59 +20,119 @@ P = 128
 T = 4
 G = C // 512
 NC = CELLS // P
+N_UNITS = B * HI * T
 FLOPS = 2 * B * HI * W * C * O + 2 * B * CELLS * W * ND + 2 * B * CELLS * W * O
+
+S = {"fix":54,"hand":420,"bt":3,"dlat":1200,"d0":0.5,"d1":22.5,"mst":2.25,"e0":-44,"e1":-8.5,"ray":8,"rayst":1.75,"w0":9.5,"wst0":0.75,"w1":71.5,"wst1":3,"tqd":-35.5,"wid":-14,"th":2,"qd":-10,"pd":5.5,"hd":-12,"ce":-14,"cw":-13,"re":14.5,"rest":3.75,"ev":9,"HP":[4,7,8,13],"pw":680}
+
+
+def list_order(tasks, banks, arrived):
+    done = dict(arrived)
+    free = {"V": 0, "S": 0, "P": 0}
+    taken = {name: [] for name in banks}
+    lacking = {}
+    users = {}
+    open_tasks = []
+    for task in tasks:
+        missing = [k for k in task[4] if k not in done]
+        lacking[task[0]] = len(missing)
+        for k in missing:
+            users.setdefault(k, []).append(task)
+        if not missing:
+            open_tasks.append((max([done[k] for k in task[4]] + [0]), task))
+    order = []
+    while open_tasks:
+        best = None
+        for item in open_tasks:
+            ready, task = item
+            ready = max(ready, free[task[1]])
+            blocked = False
+            for pool, reader in task[6]:
+                if len(taken[pool]) >= banks[pool]:
+                    last = taken[pool][-banks[pool]]
+                    if last in done:
+                        ready = max(ready, done[last])
+                    else:
+                        blocked = True
+            if blocked:
+                continue
+            rank = (ready, task[3])
+            if best is None or rank < best[0]:
+                best = (rank, item)
+        (ready, due), item = best
+        open_tasks.remove(item)
+        key, engine, work, due, after, call, holds = item[1]
+        free[engine] = ready + work + S["fix"]
+        done[key] = free[engine] + S["hand"]
+        for pool, reader in holds:
+            taken[pool].append(reader)
+        for task in users.get(key, []):
+            lacking[task[0]] -= 1
+            if lacking[task[0]] == 0:
+                open_tasks.append((max(done[k] for k in task[4]), task))
+        order.append(call)
+    assert len(order) == len(tasks)
+    return order
 
 
 def tile_matrixvtringraybev_w4_kernel(tc, x_bytes, x_scale, wc_words, wc_scales, gw, dl, gd, ring_words, ring_scales, ray, out):
     nc = tc.nc
     with ExitStack() as ctx:
         keep = ctx.enter_context(tc.tile_pool(name="keep", bufs=1))
-        per_b = ctx.enter_context(tc.tile_pool(name="per_b", bufs=2))
-        raws = ctx.enter_context(tc.tile_pool(name="raws", bufs=8))
-        flow = ctx.enter_context(tc.tile_pool(name="flow", bufs=3))
+        flow = ctx.enter_context(tc.tile_pool(name="flow", bufs=4))
         stores = ctx.enter_context(tc.tile_pool(name="stores", bufs=8))
-        ps_t = ctx.enter_context(tc.psum_pool(name="ps_t", bufs=3))
-        ps_y = ctx.enter_context(tc.psum_pool(name="ps_y", bufs=5))
+        ps_t = ctx.enter_context(tc.psum_pool(name="ps_t", bufs=S["bt"]))
+        ps_y = ctx.enter_context(tc.psum_pool(name="ps_y", bufs=8 - S["bt"]))
         ctx.enter_context(tc.manual_schedule())
 
-        warm = keep.tile([P, 1], F32, name="warm")
+        def hold(name, shape, dtype):
+            return keep.tile([P] + shape, dtype, name=name, align_bytes=64)
+
+        def hold_each(name, n, shape, dtype):
+            return [keep.tile([P] + shape, dtype, name="%s%d" % (name, i), align_bytes=64) for i in range(n)]
+
+        warm = hold("warm", [1], F32)
+        warm_out = hold("warm_out", [1], F32)
         nc.vector.memset(warm[:], 0.0)
-        warm_out = keep.tile([P, 1], F32, name="warm_out")
         nc.scalar.activation(out=warm_out[:], in_=warm[:], func=ACT.Exp)
 
-        ident = keep.tile([P, P], F32, name="ident", align_bytes=64)
+        ident = hold("ident", [P], F32)
         make_identity(nc, ident[:])
-        w_planes = keep.tile([P, G * O + CELLS], U8, name="w_planes", align_bytes=64)
+        w_planes = hold("w_planes", [G * O + CELLS], U8)
         nc.gpsimd.memset(w_planes[:].bitcast(I32), 0)
 
-        sc8 = keep.tile([P, 8], F32, name="sc8")
-        nc.scalar.dma_start(out=sc8[:], in_=x_scale.rearrange("a b c (p j) -> p (a b c j)", p=P))
-        gd4 = keep.tile([P, 4], BF16, name="gd4")
+        scol = hold("scol", [G, T], F32)
+        nc.scalar.dma_start(out=scol[:], in_=x_scale.rearrange("a b c (j p t) -> p (a b c j) t", p=P, t=T))
+        gd4 = hold("gd4", [T], BF16)
         nc.scalar.dma_start(out=gd4[:], in_=gd.rearrange("(p j) -> p j", p=P))
-        gw4 = keep.tile([P, 4], BF16, name="gw4")
+        gw4 = hold("gw4", [T], BF16)
         nc.scalar.dma_start(out=gw4[:], in_=gw.rearrange("(p j) -> p j", p=P))
 
-        dls = []
-        raw = []
-        for b in range(B):
-            dl_b = per_b.tile([P, T, ND], BF16, name="dl_b", align_bytes=64)
-            dls.append(dl_b)
-        for i in range(B * HI):
-            raw_i = raws.tile([P, T, C], U8, name="raw_i", align_bytes=64)
-            raw.append(raw_i)
-        wc = keep.tile([P, G, 2 * O], U8, name="wc", align_bytes=64)
-        ring = keep.tile([P, 2 * CELLS], U8, name="ring", align_bytes=64)
-        ray_raw = keep.tile([P, NC, W], BF16, name="ray_raw", align_bytes=64)
+        dls = hold_each("dl", B, [T, ND], BF16)
+        raw = hold_each("raw", B * HI, [T, C], U8)
+        wc = hold("wc", [G, 2 * O], U8)
+        ring = hold("ring", [2 * CELLS], U8)
+        ray_raw = hold("ray_raw", [NC, W], BF16)
+        arrived = {}
+        loaded = [0]
+
+        def load(key, dst, src, size):
+            nc.sync.dma_start(out=dst, in_=src)
+            loaded[0] += size
+            arrived[key] = S["dlat"] + loaded[0] // 4
 
         def load_dl(b):
-            nc.sync.dma_start(out=dls[b][:], in_=dl[b].rearrange("(p t) n -> p t n", t=T))
+            load(("dl", b), dls[b][:], dl[b].rearrange("(p t) n -> p t n", t=T), 2 * T * ND)
 
         def load_x(i, t0, t1):
             src = x_bytes[i // HI, i % HI].rearrange("(p t) c -> p t c", t=T)
-            nc.sync.dma_start(out=raw[i][:, t0:t1, :], in_=src[:, t0:t1, :])
+            load(("x", i, t0), raw[i][:, t0:t1, :], src[:, t0:t1, :], (t1 - t0) * C)
+            for t in range(t0, t1):
+                arrived["x", i, t] = arrived["x", i, t0]
 
         load_dl(0)
         load_x(0, 0, 1)
+        load_dl(1)
         load_x(0, 1, 4)
         for q in range(4):
             rows = slice(32 * q, 32 * q + 4)
@@ -86,71 +146,80 @@ def tile_matrixvtringraybev_w4_kernel(tc, x_bytes, x_scale, wc_words, wc_scales,
                 out=w_planes[rows, G * O :].bitcast(I32),
                 in_=ring_scales[0, 4 * q : 4 * q + 4, :].bitcast(I32),
             )
-        nc.sync.dma_start(out=wc[:].bitcast(I32), in_=wc_words.bitcast(I32).rearrange("g p n -> p g n"))
+        load("wc", wc[:].bitcast(I32), wc_words.bitcast(I32).rearrange("g p n -> p g n"), 2 * G * O)
         load_x(1, 0, 4)
-        nc.sync.dma_start(out=ray_raw[:], in_=ray.rearrange("(c p) w -> p c w", p=P))
-        nc.sync.dma_start(out=ring[:].bitcast(I32), in_=ring_words[0].bitcast(I32))
-        load_dl(1)
+        load("ray", ray_raw[:], ray.rearrange("(c p) w -> p c w", p=P), 2 * NC * W)
+        load("ring", ring[:].bitcast(I32), ring_words[0].bitcast(I32), 2 * CELLS)
         for i in range(2, B * HI):
             load_x(i, 0, 4)
 
-        scale = keep.tile([P, C], F32, name="scale", align_bytes=64)
-        gd512 = keep.tile([P, ND], F32, name="gd512", align_bytes=64)
-        gd4f = keep.tile([P, 4], F32, name="gd4f")
-        gwf = keep.tile([P, 4], F32, name="gwf")
-        gwn = keep.tile([P, 4], F32, name="gwn")
+        tasks = []
 
-        def spread_scale(j):
-            xt = ps_t.tile([P, 4, P], F32, name="xt")
-            for c in range(4):
-                col = 4 * j + c
-                nc.tensor.transpose(xt[:, c, :], sc8[:, col : col + 1].to_broadcast([P, P]), ident[:])
-            nc.scalar.copy(
-                out=scale[:].rearrange("p (n c) -> p n c", c=8)[:, :, 4 * j : 4 * j + 4],
-                in_=xt[:].rearrange("p c n -> p n c"),
-            )
+        def task(key, engine, work, due, after, call, *holds):
+            tasks.append((key, engine, work, due, after, call, holds))
+
+        def words(tile_view, pattern):
+            return tile_view.rearrange(pattern).bitcast(F32)
+
+        def turn_words(rows, dst):
+            for u in range(2):
+                nc.tensor.transpose(dst[:, u, :], rows[:, u::2], ident[:])
+
+        banks = {"turns": S["bt"], "sums": 8 - S["bt"], "rows": 4, "wide": 4, "groups": 5, "codes": 5, "halves": 2}
+
+        scale = hold("scale", [C], F32)
+        gd512 = hold("gd512", [ND], F32)
+        gd4f = hold("gd4f", [T], F32)
+        gwf = hold("gwf", [T], F32)
+        gwn = hold("gwn", [T], F32)
+        spread = {}
+
+        def spread_turn(name, cols):
+            xt = ps_t.tile([P, T, P], F32, name="xt")
+            for t in range(T):
+                nc.tensor.transpose(xt[:, t, :], cols[:, t : t + 1].to_broadcast([P, P]), ident[:])
+            spread[name] = xt
+
+        def spread_copy(name, dst):
+            nc.scalar.copy(out=dst.rearrange("p (n t) -> p n t", t=T), in_=spread[name][:].rearrange("p t n -> p n t"))
 
         def small_vectors():
             nc.vector.tensor_scalar(out=gd4f[:], in0=gd4[:], scalar1=float(ND), scalar2=None, op0=ALU.mult)
             nc.vector.tensor_copy(out=gwf[:], in_=gw4[:])
             nc.vector.tensor_scalar(out=gwn[:], in0=gw4[:], scalar1=-1.0 / O, scalar2=None, op0=ALU.mult)
 
-        def spread_gd():
-            xt = ps_t.tile([P, 4, P], F32, name="xt")
-            for c in range(4):
-                nc.tensor.transpose(xt[:, c, :], gd4f[:, c : c + 1].to_broadcast([P, P]), ident[:])
-            nc.scalar.copy(out=gd512[:].rearrange("p (n c) -> p n c", c=4), in_=xt[:].rearrange("p c n -> p n c"))
+        arrived["small"] = S["dlat"] + 300
+        task("small_v", "V", 60, 0, ["small"], small_vectors)
+        for j in range(G):
+            task(("st", j), "P", S["pw"], -2, ["small"], lambda j=j: spread_turn(j, scol[:, j, :]), ("turns", ("sc", j)))
+            task(("sc", j), "S", 512, -2, [("st", j)], lambda j=j: spread_copy(j, scale[:, 512 * j : 512 * (j + 1)]))
+        task("gt", "P", S["pw"], -1, ["small_v"], lambda: spread_turn("gd", gd4f), ("turns", "gc"))
+        task("gc", "S", 512, -1, ["gt"], lambda: spread_copy("gd", gd512[:]))
 
-        negmax, esum, rsum, e_t, d_t, dg, d_codes, d_planes = {}, {}, {}, {}, {}, {}, {}, {}
-        tmg, tm_codes, tm_planes = {}, {}, {}
-        ray_t = keep.tile([P, NC, P, T], BF16, name="ray_t", align_bytes=64)
+        m1 = hold_each("m1_", B, [T, ND // 2], BF16)
+        m2 = hold_each("m2_", B, [T, ND // 4], BF16)
+        mx = hold_each("mx", B, [T], F32)
+        negmax = hold_each("negmax", B, [T], F32)
+        esum = hold_each("esum", B, [T], F32)
+        rsum = hold_each("rsum", B, [T], F32)
+        e_t = hold_each("e", B, [T, ND], F32)
+        d_t = hold_each("d", B, [T, ND], BF16)
+        dg = hold_each("dg", B, [T, P, T], BF16)
+        d_codes = hold_each("dcodes", B, [W], U32)
+        d_planes = hold_each("dplanes", B, [W], U8)
+        turned = {}
 
-        m1, m2, mx = {}, {}, {}
+        def d_max_1(b):
+            nc.vector.tensor_max(out=m1[b][:], in0=dls[b][:, :, 0 : ND // 2], in1=dls[b][:, :, ND // 2 :])
 
-        def d_max_step(b, k):
-            if k == 0:
-                m1[b] = per_b.tile([P, T, ND // 2], BF16, name="m1_b")
-                m2[b] = per_b.tile([P, T, ND // 4], BF16, name="m2_b")
-                mx[b] = per_b.tile([P, T], F32, name="mx_b")
-                negmax[b] = per_b.tile([P, T], F32, name="negmax_b")
-                esum[b] = per_b.tile([P, T], F32, name="esum_b")
-                nc.vector.tensor_max(out=m1[b][:], in0=dls[b][:, :, 0 : ND // 2], in1=dls[b][:, :, ND // 2 :])
-            elif k == 1:
-                nc.vector.tensor_max(out=m2[b][:], in0=m1[b][:, :, 0 : ND // 4], in1=m1[b][:, :, ND // 4 :])
-            elif k == 2:
-                nc.vector.reduce_max(out=mx[b][:], in_=m2[b][:], axis=AXIS.X)
-            else:
-                nc.vector.tensor_scalar(out=negmax[b][:], in0=mx[b][:], scalar1=-1.0, scalar2=None, op0=ALU.mult)
-                d_tiles(b)
+        def d_max_2(b):
+            nc.vector.tensor_max(out=m2[b][:], in0=m1[b][:, :, 0 : ND // 4], in1=m1[b][:, :, ND // 4 :])
 
-        def d_tiles(b):
-            e_t[b] = per_b.tile([P, T, ND], F32, name="e_b", align_bytes=64)
-            d_t[b] = per_b.tile([P, T, ND], BF16, name="d_b", align_bytes=64)
-            dg[b] = per_b.tile([P, T, P, T], BF16, name="dg_b", align_bytes=64)
-            d_codes[b] = per_b.tile([P, W], U32, name="dcodes_b", align_bytes=64)
-            d_planes[b] = per_b.tile([P, W], U8, name="dplanes_b", align_bytes=64)
-            tm_codes[b] = per_b.tile([P, CELLS], U32, name="tmcodes_b", align_bytes=64)
-            tm_planes[b] = per_b.tile([P, CELLS], U8, name="tmplanes_b", align_bytes=64)
+        def d_max_3(b):
+            nc.vector.reduce_max(out=mx[b][:], in_=m2[b][:], axis=AXIS.X)
+
+        def d_max_4(b):
+            nc.vector.tensor_scalar(out=negmax[b][:], in0=mx[b][:], scalar1=-1.0, scalar2=None, op0=ALU.mult)
 
         def d_exp(b, t):
             nc.scalar.activation(
@@ -158,7 +227,6 @@ def tile_matrixvtringraybev_w4_kernel(tc, x_bytes, x_scale, wc_words, wc_scales,
             )
 
         def d_recip(b):
-            rsum[b] = per_b.tile([P, T], F32, name="rsum_b")
             nc.vector.reciprocal(out=rsum[b][:], in_=esum[b][:])
 
         def d_mul(b, t):
@@ -166,39 +234,47 @@ def tile_matrixvtringraybev_w4_kernel(tc, x_bytes, x_scale, wc_words, wc_scales,
                 out=d_t[b][:, t, :], in0=e_t[b][:, t, :], scalar=rsum[b][:, t : t + 1], in1=gd512[:], op0=ALU.mult, op1=ALU.mult
             )
 
-        turned = {}
-
-        def turn_pair(key, words, first):
+        def turn_pair(key, rows_of):
             xt = ps_t.tile([P, 2, 2, P], F32, name="xt")
             for j in range(2):
-                for u in range(2):
-                    start = 256 * (first + j)
-                    nc.tensor.transpose(xt[:, j, u, :], words[:, start + u : start + 256 : 2], ident[:])
+                turn_words(rows_of(j), xt[:, j])
             turned[key] = xt
 
         def untangle(key, dst):
             nc.scalar.copy(
-                out=dst.rearrange("p j n k -> p (j n k)").bitcast(F32).rearrange("p (j n u) -> p j n u", j=2, u=2),
+                out=words(dst, "p j n k -> p (j n k)").rearrange("p (j n u) -> p j n u", j=2, u=2),
                 in_=turned[key][:].rearrange("p j u n -> p j n u"),
             )
-
-        def d_turn(b, h):
-            turn_pair(("d", b, h), d_t[b][:].rearrange("p t n -> p (t n)").bitcast(F32), 2 * h)
-
-        def d_copy(b, h):
-            untangle(("d", b, h), dg[b][:, 2 * h : 2 * h + 2, :, :])
 
         def d_quant(b):
             nc.vector.quantize_mx(
                 out=d_codes[b][:].bitcast(FP8X4), scales=d_planes[b][:], in_=dg[b][:].rearrange("p t w k -> p (t w k)")
             )
 
-        def ray_turn(i):
-            turn_pair(("ray", i), ray_raw[:].rearrange("p c w -> p (c w)").bitcast(F32), 2 * i)
+        for b in range(B):
+            due = S["d%d" % b]
+            task(("dm", b, 1), "V", 512, -8 + b, [("dl", b)], lambda b=b: d_max_1(b))
+            task(("dm", b, 2), "V", 256, -7 + b, [("dm", b, 1)], lambda b=b: d_max_2(b))
+            task(("dm", b, 3), "V", 512, -6 + b, [("dm", b, 2)], lambda b=b: d_max_3(b))
+            task(("dm", b, 4), "V", 10, -5 + b, [("dm", b, 3)], lambda b=b: d_max_4(b))
+            for t in range(T):
+                task(("de", b, t), "S", 560, S["e%d" % b], [("dm", b, 4)], lambda b=b, t=t: d_exp(b, t))
+            task(("dr", b), "V", 40, due, [("de", b, t) for t in range(T)], lambda b=b: d_recip(b))
+            for t in range(T):
+                task(("du", b, t), "V", 512, due + S["mst"] * t, [("dr", b), "gc"], lambda b=b, t=t: d_mul(b, t))
+            for h in range(2):
+                task(
+                    ("dt", b, h), "P", S["pw"], due, [("du", b, 2 * h), ("du", b, 2 * h + 1)],
+                    lambda b=b, h=h: turn_pair(("d", b, h), lambda j: words(d_t[b][:, 2 * h + j : 2 * h + j + 1, :], "p t n -> p (t n)")),
+                    ("turns", ("dc", b, h)),
+                )
+                task(("dc", b, h), "S", 512, due, [("dt", b, h)], lambda b=b, h=h: untangle(("d", b, h), dg[b][:, 2 * h : 2 * h + 2, :, :]))
+            task(("dq", b), "V", 512, due + 2, [("dc", b, 0), ("dc", b, 1)], lambda b=b: d_quant(b))
 
-        def ray_copy(i):
-            untangle(("ray", i), ray_t[:, 2 * i : 2 * i + 2, :, :])
-
+        ray_t = hold("ray_t", [NC, P, T], BF16)
+        tmg = [hold("tmg", [NC, P, T], BF16)] * B
+        tm_codes = hold_each("tmcodes", B, [CELLS], U32)
+        tm_planes = hold_each("tmplanes", B, [CELLS], U8)
         rds = {}
 
         def transport(b, c):
@@ -216,59 +292,104 @@ def tile_matrixvtringraybev_w4_kernel(tc, x_bytes, x_scale, wc_words, wc_scales,
             rds[b, c] = rd
 
         def weigh(b, c):
-            rd = rds[b, c]
-            if c % 4 == 0:
-                tmg[b, c // 4] = per_b.tile([P, 4, P, T], BF16, name="tmg_b", align_bytes=64)
             nc.vector.tensor_tensor(
-                out=tmg[b, c // 4][:, c % 4, :, :], in0=rd[:].rearrange("p t n -> p n t"), in1=ray_t[:, c, :, :], op=ALU.mult
+                out=tmg[b][:, c, :, :], in0=rds[b, c][:].rearrange("p t n -> p n t"), in1=ray_t[:, c, :, :], op=ALU.mult
             )
 
-        def tm_quant(b, h):
+        def tm_quant(b, c, n):
             nc.vector.quantize_mx(
-                out=tm_codes[b][:, 512 * h : 512 * (h + 1)].bitcast(FP8X4),
-                scales=tm_planes[b][:, 512 * h : 512 * (h + 1)],
-                in_=tmg[b, h][:].rearrange("p c n k -> p (c n k)"),
+                out=tm_codes[b][:, P * c : P * (c + n)].bitcast(FP8X4),
+                scales=tm_planes[b][:, P * c : P * (c + n)],
+                in_=tmg[b][:, c : c + n, :, :].rearrange("p c n k -> p (c n k)"),
             )
 
-        n_units = B * HI * T
-        xs, xg, x_codes, x_planes, y_ps, m_t, msum, ctxg, c_codes, c_planes = {}, {}, {}, {}, {}, {}, {}, {}, {}, {}
+        for i in range(NC // 2):
+            due = S["ray"] + S["rayst"] * i
+            task(
+                ("rt", i), "P", S["pw"], due, ["ray"],
+                lambda i=i: turn_pair(("ray", i), lambda j: words(ray_raw[:, 2 * i + j : 2 * i + j + 1, :], "p c w -> p (c w)")),
+                ("turns", ("rc", i)),
+            )
+            task(("rc", i), "S", 512, due, [("rt", i)], lambda i=i: untangle(("ray", i), ray_t[:, 2 * i : 2 * i + 2, :, :]))
+        for b in range(B):
+            for c in range(NC):
+                due = S["w%d" % b] + S["wst%d" % b] * c
+                task(("tr", b, c), "P", S["pw"] // 2, due - 1, [("dq", b), "ring"], lambda b=b, c=c: transport(b, c), ("sums", ("we", b, c)))
+                task(("we", b, c), "V", 512, due, [("tr", b, c), ("rc", c // 2)] + ([("tq", b - 1, c // 2)] if b else []), lambda b=b, c=c: weigh(b, c))
+                if c % 2 == 1:
+                    task(("tq", b, c // 2), "V", 256, due + S["tqd"], [("we", b, c - 1), ("we", b, c)], lambda b=b, c=c: tm_quant(b, c - 1, 2))
+
+        m_t = hold_each("m", B, [T, O], F32)
+        msum = hold_each("msum", B, [T], F32)
+        bias = hold_each("bias", B, [T], F32)
+        ctxp = [hold("ctxp", [2, O, 2], BF16)] * B
+        ctxg = [hold("ctxg", [O, T], BF16)] * B
+        c_codes = hold_each("ccodes", B, [O], U32)
+        c_planes = hold_each("cplanes", B, [O], U8)
+        xs, xg, x_codes, x_planes, halves, y_ps, accs = {}, {}, {}, {}, {}, {}, {}
+
+        def group_tiles(s):
+            xg[s] = flow.tile([P, G, 2, P, T], BF16, name="xg_s", align_bytes=64, bufs=banks["groups"])
+            x_codes[s] = flow.tile([P, G, 2, P], U32, name="xcodes_s", align_bytes=64, bufs=banks["codes"])
+            x_planes[s] = flow.tile([P, G, 2, P], U8, name="xplanes_s", align_bytes=64, bufs=banks["codes"])
 
         def scale_rows(q):
-            i, t = divmod(q, T)
-            xs[q] = flow.tile([P, C], BF16, name="xs_q", align_bytes=64)
-            nc.vector.tensor_tensor(out=xs[q][:], in0=raw[i][:, t, :].bitcast(F8), in1=scale[:], op=ALU.mult)
+            if q % 2 == 0:
+                group_tiles(q // 2)
+            xs[q] = flow.tile([P, C], BF16, name="xs_q", align_bytes=64, bufs=banks["rows"])
+            nc.vector.tensor_tensor(out=xs[q][:], in0=raw[q // T][:, q % T, :].bitcast(F8), in1=scale[:], op=ALU.mult)
+
+        def widen(q):
+            xs[q] = flow.tile([P, C], BF16, name="xw_q", align_bytes=64, bufs=banks["wide"])
+            nc.scalar.copy(out=xs[q][:], in_=raw[q // T][:, q % T, :].bitcast(F8))
 
         def turn(q):
-            pair, k = divmod(q, 2)
-            if k == 0:
-                xg[pair] = flow.tile([P, 2, G, P, T], BF16, name="xg_p", align_bytes=64)
-                x_codes[pair] = flow.tile([P, 2, G, P], U32, name="xcodes_p", align_bytes=64)
-                x_planes[pair] = flow.tile([P, 2, G, P], U8, name="xplanes_p", align_bytes=64)
-            xt = ps_t.tile([P, G, 2, P], F32, name="xt")
-            words = xs[q][:].bitcast(F32)
-            for g in range(G):
-                for u in range(2):
-                    nc.tensor.transpose(xt[:, g, u, :], words[:, 256 * g + u : 256 * (g + 1) : 2], ident[:])
+            turn_pair(("x", q), lambda g: xs[q][:, 512 * g : 512 * (g + 1)].bitcast(F32))
+
+        def turn_copy(q):
+            s, k = divmod(q, 2)
             nc.scalar.copy(
-                out=xg[pair][:, k].rearrange("p g r k -> p (g r k)").bitcast(F32).rearrange("p (g r u) -> p g r u", g=G, u=2),
-                in_=xt[:].rearrange("p g u r -> p g r u"),
+                out=xg[s][:].rearrange("p g k r t -> p (g k r t)").bitcast(F32).rearrange("p (g k r u) -> p g k r u", g=G, k=2, u=2)[:, :, k],
+                in_=turned["x", q][:].rearrange("p g u r -> p g r u"),
             )
 
-        def quant(pair, k0, k1):
+        def turn_pass(s, g):
+            if g == 0:
+                halves[s] = flow.tile([P, G, 2, 2 * P, 2], BF16, name="halves_s", align_bytes=64, bufs=banks["halves"])
+            turn_pair(("h", s, g), lambda k: xs[2 * s + k][:, 512 * g : 512 * (g + 1)].bitcast(F32))
+
+        def scale_turned(s, g, u):
+            values = turned["h", s, g][:].rearrange("p k u r -> p (k u r)").bitcast(BF16).rearrange("p (k u r e) -> p k u r e", k=2, u=2, e=2)
+            for e in range(2):
+                nc.scalar.activation(
+                    out=halves[s][:, g, u, :, e].rearrange("p (k r) -> p k r", k=2),
+                    in_=values[:, :, u, :, e],
+                    func=ACT.Copy,
+                    scale=scol[:, g, 2 * u + e : 2 * u + e + 1],
+                )
+
+        def weave(s):
+            group_tiles(s)
+            nc.vector.tensor_copy(
+                out=words(xg[s][:], "p g k r t -> p (g k r t)").rearrange("p (g c u) -> p g c u", g=G, u=2),
+                in_=words(halves[s][:], "p g u c e -> p (g u c e)").rearrange("p (g u c) -> p g c u", g=G, u=2),
+            )
+
+        def quant(s):
             nc.vector.quantize_mx(
-                out=x_codes[pair][:, k0:k1].rearrange("p k g r -> p (k g r)").bitcast(FP8X4),
-                scales=x_planes[pair][:, k0:k1].rearrange("p k g r -> p (k g r)"),
-                in_=xg[pair][:, k0:k1].rearrange("p k g r j -> p (k g r j)"),
+                out=x_codes[s][:].rearrange("p g k r -> p (g k r)").bitcast(FP8X4),
+                scales=x_planes[s][:].rearrange("p g k r -> p (g k r)"),
+                in_=xg[s][:].rearrange("p g k r t -> p (g k r t)"),
             )
 
         def project(q):
-            pair, k = divmod(q, 2)
+            s, k = divmod(q, 2)
             y_ps[q] = ps_y.tile([P, O], F32, name="acc")
             for g in range(G):
                 nc.tensor.matmul_mx(
                     out=y_ps[q][:],
-                    lhsT=x_codes[pair][:, k, g, :].bitcast(FP8X4),
-                    lhsT_scale=x_planes[pair][:, k, g, :],
+                    lhsT=x_codes[s][:, g, k, :].bitcast(FP8X4),
+                    lhsT_scale=x_planes[s][:, g, k, :],
                     rhs=wc[:, g, :].bitcast(FP4X4),
                     rhs_scale=w_planes[:, O * g : O * (g + 1)],
                     start=(g == 0),
@@ -278,12 +399,6 @@ def tile_matrixvtringraybev_w4_kernel(tc, x_bytes, x_scale, wc_words, wc_scales,
         def height_max(q):
             i, t = divmod(q, T)
             b, h = divmod(i, HI)
-            if h == 0 and t == 0:
-                m_t[b] = per_b.tile([P, T, O], F32, name="m_b", align_bytes=64)
-                msum[b] = per_b.tile([P, T], F32, name="msum_b")
-                ctxg[b] = per_b.tile([P, O, T], BF16, name="ctxg_b", align_bytes=64)
-                c_codes[b] = per_b.tile([P, O], U32, name="ccodes_b", align_bytes=64)
-                c_planes[b] = per_b.tile([P, O], U8, name="cplanes_b", align_bytes=64)
             m = m_t[b][:, t, :]
             if h == 0:
                 nc.scalar.copy(out=m, in_=y_ps[q][:])
@@ -295,18 +410,21 @@ def tile_matrixvtringraybev_w4_kernel(tc, x_bytes, x_scale, wc_words, wc_scales,
                 )
 
         def centre(b, t):
-            bias = per_b.tile([P, 1], F32, name="bias")
-            nc.scalar.activation(out=bias[:], in_=msum[b][:, t : t + 1], func=ACT.Copy, scale=gwn[:, t : t + 1])
+            nc.scalar.activation(out=bias[b][:, t : t + 1], in_=msum[b][:, t : t + 1], func=ACT.Copy, scale=gwn[:, t : t + 1])
             nc.scalar.activation(
-                out=ctxg[b][:, :, t], in_=m_t[b][:, t, :], func=ACT.Identity, scale=gwf[:, t : t + 1], bias=bias[:]
+                out=ctxp[b][:, t // 2, :, t % 2], in_=m_t[b][:, t, :], func=ACT.Identity, scale=gwf[:, t : t + 1], bias=bias[b][:, t : t + 1]
+            )
+
+        def ctx_weave(b):
+            nc.vector.tensor_copy(
+                out=words(ctxg[b][:], "p o t -> p (o t)").rearrange("p (o u) -> p o u", u=2),
+                in_=words(ctxp[b][:], "p u o e -> p (u o e)").rearrange("p (u o) -> p o u", u=2),
             )
 
         def ctx_quant(b):
             nc.vector.quantize_mx(
                 out=c_codes[b][:].bitcast(FP8X4), scales=c_planes[b][:], in_=ctxg[b][:].rearrange("p o t -> p (o t)")
             )
-
-        accs = {}
 
         def result(b, c):
             acc = ps_y.tile([P, O], F32, name="acc")
@@ -321,113 +439,53 @@ def tile_matrixvtringraybev_w4_kernel(tc, x_bytes, x_scale, wc_words, wc_scales,
             )
             accs[b, c] = acc
 
-        def emit(b, c, on_vector):
-            acc = accs[b, c]
+        def emit(b, c, engine):
             res = stores.tile([P, O], F32, name="res", align_bytes=64)
-            if on_vector:
-                nc.vector.tensor_copy(out=res[:], in_=acc[:])
+            if engine == "V":
+                nc.vector.tensor_copy(out=res[:], in_=accs[b, c][:])
             else:
-                nc.scalar.copy(out=res[:], in_=acc[:])
+                nc.scalar.copy(out=res[:], in_=accs[b, c][:])
             nc.sync.dma_start(out=out[b, P * c : P * (c + 1), :], in_=res[:])
 
-        pe, act, vec = {}, {}, {}
+        for s in range(N_UNITS // 2):
+            pair = (2 * s, 2 * s + 1)
+            if s in S["HP"]:
+                for q in pair:
+                    task(("tt", q), "S", 1024, q - S["wid"], [("x", q // T, q % T)], lambda q=q: widen(q), ("wide", ("tp", s, 1)))
+                for g in range(G):
+                    due = 2 * s - S["th"] + 2 * g
+                    task(
+                        ("tp", s, g), "P", S["pw"], due, [("tt", q) for q in pair] + ([("tp", s, 0)] if g else []), lambda s=s, g=g: turn_pass(s, g),
+                        ("turns", ("ex", s, g, 1)), *([] if g else [("halves", ("wv", s))]),
+                    )
+                    for u in range(2):
+                        task(("ex", s, g, u), "S", 780, due + u, [("tp", s, g)], lambda s=s, g=g, u=u: scale_turned(s, g, u))
+                task(("wv", s), "V", 512, 2 * s, [("ex", s, g, u) for g in range(G) for u in range(2)], lambda s=s: weave(s), ("groups", ("qu", s)), ("codes", ("pr", 2 * s + 1)))
+                ready = [("wv", s)]
+            else:
+                for q in pair:
+                    task(("tt", q), "V", 1024, q, [("x", q // T, q % T), ("sc", 0), ("sc", 1)], lambda q=q: scale_rows(q), ("rows", ("tu", q)), *([] if q % 2 else [("groups", ("qu", s)), ("codes", ("pr", q + 1))]))
+                    task(("tu", q), "P", S["pw"], q, [("tt", q)], lambda q=q: turn(q), ("turns", ("cp", q)))
+                    task(("cp", q), "S", 512, q, [("tu", q)], lambda q=q: turn_copy(q))
+                ready = [("cp", q) for q in pair]
+            task(("qu", s), "V", 512, 2 * s + S["qd"], ready, lambda s=s: quant(s))
+            for q in pair:
+                i, t = divmod(q, T)
+                b, h = divmod(i, HI)
+                task(("pr", q), "P", S["pw"], q + S["pd"], [("qu", s), "wc"], lambda q=q: project(q), ("sums", ("hm", q)))
+                engine = "S" if h == 0 else "V"
+                before = [("hm", q - T)] if h else []
+                task(("hm", q), engine, 512, q + S["hd"], [("pr", q)] + before, lambda q=q: height_max(q))
+        for b in range(B):
+            for t in range(T):
+                task(("ce", b, t), "S", 900, S["ce"] + 16 * b, [("hm", (b * HI + HI - 1) * T + t)] + ([("cw", b - 1)] if b else []), lambda b=b, t=t: centre(b, t))
+            task(("cw", b), "V", 512, S["cw"] + 13 * b, [("ce", b, t) for t in range(T)] + ([("cq", b - 1)] if b else []), lambda b=b: ctx_weave(b))
+            task(("cq", b), "V", 512, S["cw"] + 13 * b, [("cw", b)], lambda b=b: ctx_quant(b))
+            for c in range(NC):
+                engine = "V" if b == 1 and c >= S["ev"] and c % 2 == 1 else "S"
+                due = S["re"] + c * S["rest"] + 20 * b
+                task(("re", b, c), "P", S["pw"] // 2, due, [("cq", b), ("tq", b, c // 2)], lambda b=b, c=c: result(b, c), ("sums", ("em", b, c)))
+                task(("em", b, c), engine, 512, due, [("re", b, c)], lambda b=b, c=c, engine=engine: emit(b, c, engine))
 
-        def at(table, q, fn, *args):
-            table.setdefault(q, []).append((fn, args))
-
-        def run(table, q):
-            for fn, args in table.get(q, []):
-                fn(*args)
-
-        at(vec, 1, d_recip, 0)
-        for t in range(T):
-            at(vec, 2 + t // 2, d_mul, 0, t)
-        for h in range(2):
-            at(pe, 3 + h, d_turn, 0, h)
-            at(act, 4 + h, d_copy, 0, h)
-        at(vec, 7, d_quant, 0)
-        for i in range(4):
-            at(pe, 5 + i, ray_turn, i)
-            at(act, 6 + i, ray_copy, i)
-        for c in range(NC):
-            at(pe, 8 + c, transport, 0, c)
-            at(vec, 10 + c, weigh, 0, c)
-        at(vec, 14, tm_quant, 0, 0)
-        at(vec, 18, tm_quant, 0, 1)
-        for k in range(4):
-            at(vec, 4 + k, d_max_step, 1, k)
-        for t in range(T):
-            at(act, 10 + t, d_exp, 1, t)
-        at(vec, 15, d_recip, 1)
-        for t in range(T):
-            at(vec, 16 + t, d_mul, 1, t)
-        for h in range(2):
-            at(pe, 19 + 2 * h, d_turn, 1, h)
-            at(act, 20 + 2 * h, d_copy, 1, h)
-        at(vec, 23, d_quant, 1)
-        for t in range(T):
-            at(act, 19 + t, centre, 0, t)
-        at(vec, 24, ctx_quant, 0)
-        for c in range(NC - 1):
-            at(pe, 25 + c, result, 0, c)
-            at(act, 26 + c, emit, 0, c, False)
-        for c in range(3):
-            at(pe, 25 + 2 * c, transport, 1, c)
-            at(vec, 27 + 2 * c, weigh, 1, c)
-
-        for k in range(4):
-            d_max_step(0, k)
-        small_vectors()
-        for j in range(2):
-            spread_scale(j)
-        for t in range(T):
-            d_exp(0, t)
-        spread_gd()
-        for q in range(n_units):
-            if q >= 4:
-                project(q - 4)
-            run(pe, q)
-            run(act, q)
-            run(vec, q)
-            if q >= 6:
-                height_max(q - 6)
-            scale_rows(q)
-            turn(q)
-            if q >= 3 and q % 2 == 1:
-                quant((q - 3) // 2, 0, 2)
-        last = n_units - 1
-        project(last - 3)
-        emit(0, NC - 2, False)
-        height_max(last - 5)
-        quant(last // 2, 0, 1)
-        project(last - 2)
-        height_max(last - 4)
-        result(0, NC - 1)
-        project(last - 1)
-        height_max(last - 3)
-        emit(0, NC - 1, False)
-        centre(1, 0)
-        transport(1, 3)
-        quant(last // 2, 1, 2)
-        project(last)
-        height_max(last - 2)
-        centre(1, 1)
-        transport(1, 4)
-        weigh(1, 3)
-        height_max(last - 1)
-        centre(1, 2)
-        transport(1, 5)
-        tm_quant(1, 0)
-        height_max(last)
-        centre(1, 3)
-        weigh(1, 4)
-        transport(1, 6)
-        weigh(1, 5)
-        transport(1, 7)
-        weigh(1, 6)
-        weigh(1, 7)
-        ctx_quant(1)
-        tm_quant(1, 1)
-        for c in range(NC):
-            result(1, c)
-            emit(1, c, c % 2 == 1)
+        for call in list_order(tasks, banks, arrived):
+            call()

@@ -13,33 +13,76 @@ FP8X4 = mybir.dt.float8_e4m3fn_x4
 FP4X4 = mybir.dt.float4_e2m1fn_x4
 ALU = mybir.AluOpType
 ACT = mybir.ActivationFunctionType
-AXIS = mybir.AxisListType
 
 B, HI, W, C, ND, CELLS, O = 2, 4, 512, 1024, 512, 1024, 512
 P = 128
-T = 4
-G = C // 512
-NC = CELLS // P
-N_UNITS = B * HI * T
+PACK = 4
+K_PASS = P * PACK
+G = C // K_PASS
+CHUNKS = CELLS // P
+N_UNITS = B * HI * PACK
 FLOPS = 2 * B * HI * W * C * O + 2 * B * CELLS * W * ND + 2 * B * CELLS * W * O
 
-S = {"fix":54,"hand":420,"bt":3,"dlat":1200,"d0":0.5,"d1":22.5,"mst":2.25,"e0":-44,"e1":-8.5,"ray":8,"rayst":1.75,"w0":9.5,"wst0":0.75,"w1":71.5,"wst1":3,"tqd":-35.5,"wid":-14,"th":2,"qd":-10,"pd":5.5,"hd":-12,"ce":-14,"cw":-13,"re":14.5,"rest":3.75,"ev":9,"HP":[4,7,8,13],"pw":680}
+SCALAR_PAIRS = (8, 9, 11, 14)
+SCALAR_WEAVES = (8, 14)
+SCALAR_CTX_WEAVES = (1,)
+VECTOR_RESULTS = (6, 7)
+
+SLOTS = {"turned": 4, "sums": 4, "rows": 4, "wide": 4, "pairs": 5, "codes": 5, "halves": 2}
+
+CALL = 60
+HANDOFF = 540
+SAME_ENGINE = 160
+LOAD_START = 1600
+TENSOR_RUN = 680
+
+DUE = {
+    "exp": (-100, -20.5),
+    "depth": (-26, 23.5),
+    "depth step": 6.5,
+    "ray": 16.5,
+    "ray step": 2,
+    "transport": (-7, 153),
+    "transport step": (4.75, 11),
+    "late transport": 80,
+    "transport codes": -30.5,
+    "widen": 15.5,
+    "pair turn": -9,
+    "quantise": -6,
+    "project": 4.5,
+    "height maximum": 8,
+    "centre": 22,
+    "centre step": 16,
+    "context": 10.5,
+    "context step": 13,
+    "result": 10.5,
+    "result step": 12.5,
+    "result batch step": 20,
+}
+LATE_CHUNK = 4
 
 
-def list_order(tasks, banks, arrived):
-    done = dict(arrived)
-    free = {"V": 0, "S": 0, "P": 0}
-    taken = {name: [] for name in banks}
+def list_order(tasks, arrived):
+    done = {key: (time, "load") for key, time in arrived.items()}
+    free = {"vector": 0, "scalar": 0, "tensor": 0, "gpsimd": 0}
+    taken = {kind: [] for kind in SLOTS}
     lacking = {}
     users = {}
     open_tasks = []
+
+    def usable(key, engine):
+        time, maker = done[key]
+        if maker == "load":
+            return time
+        return time + (SAME_ENGINE if maker == engine else HANDOFF)
+
     for task in tasks:
         missing = [k for k in task[4] if k not in done]
         lacking[task[0]] = len(missing)
         for k in missing:
             users.setdefault(k, []).append(task)
         if not missing:
-            open_tasks.append((max([done[k] for k in task[4]] + [0]), task))
+            open_tasks.append((max([usable(k, task[1]) for k in task[4]]), task))
     order = []
     while open_tasks:
         best = None
@@ -47,11 +90,11 @@ def list_order(tasks, banks, arrived):
             ready, task = item
             ready = max(ready, free[task[1]])
             blocked = False
-            for pool, reader in task[6]:
-                if len(taken[pool]) >= banks[pool]:
-                    last = taken[pool][-banks[pool]]
-                    if last in done:
-                        ready = max(ready, done[last])
+            for kind, last_use in task[6]:
+                if len(taken[kind]) >= SLOTS[kind]:
+                    previous = taken[kind][-SLOTS[kind]]
+                    if previous in done:
+                        ready = max(ready, usable(previous, task[1]))
                     else:
                         blocked = True
             if blocked:
@@ -62,27 +105,29 @@ def list_order(tasks, banks, arrived):
         (ready, due), item = best
         open_tasks.remove(item)
         key, engine, work, due, after, call, holds = item[1]
-        free[engine] = ready + work + S["fix"]
-        done[key] = free[engine] + S["hand"]
-        for pool, reader in holds:
-            taken[pool].append(reader)
+        free[engine] = ready + work + CALL
+        done[key] = (free[engine], engine)
+        for kind, last_use in holds:
+            taken[kind].append(last_use)
         for task in users.get(key, []):
             lacking[task[0]] -= 1
             if lacking[task[0]] == 0:
-                open_tasks.append((max(done[k] for k in task[4]), task))
+                open_tasks.append((max(usable(k, task[1]) for k in task[4]), task))
         order.append(call)
     assert len(order) == len(tasks)
     return order
 
 
-def tile_matrixvtringraybev_w4_kernel(tc, x_bytes, x_scale, wc_words, wc_scales, gw, dl, gd, ring_words, ring_scales, ray, out):
+def tile_matrixvtringraybev_w4_kernel(
+    tc, x_bytes, x_scale, wc_words, wc_scales, gw, dl, gd, ring_words, ring_scales, ray, out
+):
     nc = tc.nc
     with ExitStack() as ctx:
         keep = ctx.enter_context(tc.tile_pool(name="keep", bufs=1))
         flow = ctx.enter_context(tc.tile_pool(name="flow", bufs=4))
         stores = ctx.enter_context(tc.tile_pool(name="stores", bufs=8))
-        ps_t = ctx.enter_context(tc.psum_pool(name="ps_t", bufs=S["bt"]))
-        ps_y = ctx.enter_context(tc.psum_pool(name="ps_y", bufs=8 - S["bt"]))
+        psum_turned = ctx.enter_context(tc.psum_pool(name="psum_turned", bufs=SLOTS["turned"]))
+        psum_sums = ctx.enter_context(tc.psum_pool(name="psum_sums", bufs=SLOTS["sums"]))
         ctx.enter_context(tc.manual_schedule())
 
         def hold(name, shape, dtype):
@@ -91,401 +136,499 @@ def tile_matrixvtringraybev_w4_kernel(tc, x_bytes, x_scale, wc_words, wc_scales,
         def hold_each(name, n, shape, dtype):
             return [keep.tile([P] + shape, dtype, name="%s%d" % (name, i), align_bytes=64) for i in range(n)]
 
-        warm = hold("warm", [1], F32)
-        warm_out = hold("warm_out", [1], F32)
-        nc.vector.memset(warm[:], 0.0)
-        nc.scalar.activation(out=warm_out[:], in_=warm[:], func=ACT.Exp)
+        scales = hold("scales", [G, PACK], F32)
+        nc.scalar.dma_start(out=scales[:], in_=x_scale.rearrange("a b c (g p t) -> p (a b c g) t", p=P, t=PACK))
+        gd_raw = hold("gd_raw", [PACK], BF16)
+        nc.scalar.dma_start(out=gd_raw[:], in_=gd.rearrange("(p t) -> p t", p=P))
+        gw_raw = hold("gw_raw", [PACK], BF16)
+        nc.scalar.dma_start(out=gw_raw[:], in_=gw.rearrange("(p t) -> p t", p=P))
+
+        first = hold("first", [1], F32)
+        first_out = hold("first_out", [1], F32)
+        nc.vector.memset(first[:], 0.0)
+        nc.scalar.activation(out=first_out[:], in_=first[:], func=ACT.Exp)
 
         ident = hold("ident", [P], F32)
         make_identity(nc, ident[:])
-        w_planes = hold("w_planes", [G * O + CELLS], U8)
-        nc.gpsimd.memset(w_planes[:].bitcast(I32), 0)
+        w_scales = hold("w_scales", [G * O + CELLS], U8)
+        nc.gpsimd.memset(w_scales[:].bitcast(I32), 0)
 
-        scol = hold("scol", [G, T], F32)
-        nc.scalar.dma_start(out=scol[:], in_=x_scale.rearrange("a b c (j p t) -> p (a b c j) t", p=P, t=T))
-        gd4 = hold("gd4", [T], BF16)
-        nc.scalar.dma_start(out=gd4[:], in_=gd.rearrange("(p j) -> p j", p=P))
-        gw4 = hold("gw4", [T], BF16)
-        nc.scalar.dma_start(out=gw4[:], in_=gw.rearrange("(p j) -> p j", p=P))
-
-        dls = hold_each("dl", B, [T, ND], BF16)
-        raw = hold_each("raw", B * HI, [T, C], U8)
+        dl_raw = hold_each("dl_raw", B, [PACK, ND], BF16)
+        x_raw = hold_each("x_raw", B * HI, [PACK, C], U8)
         wc = hold("wc", [G, 2 * O], U8)
         ring = hold("ring", [2 * CELLS], U8)
-        ray_raw = hold("ray_raw", [NC, W], BF16)
-        arrived = {}
+        ray_raw = hold("ray_raw", [CHUNKS, W], BF16)
+        arrived = {"scales": LOAD_START, "gains": LOAD_START + 800}
         loaded = [0]
 
         def load(key, dst, src, size):
             nc.sync.dma_start(out=dst, in_=src)
             loaded[0] += size
-            arrived[key] = S["dlat"] + loaded[0] // 4
+            arrived[key] = LOAD_START + loaded[0] // 4
 
-        def load_dl(b):
-            load(("dl", b), dls[b][:], dl[b].rearrange("(p t) n -> p t n", t=T), 2 * T * ND)
+        def load_dl(b, half):
+            ts = slice(2 * half, 2 * half + 2)
+            load(("dl", b, half), dl_raw[b][:, ts, :], dl[b].rearrange("(p t) n -> p t n", t=PACK)[:, ts, :], 4 * ND)
 
         def load_x(i, t0, t1):
-            src = x_bytes[i // HI, i % HI].rearrange("(p t) c -> p t c", t=T)
-            load(("x", i, t0), raw[i][:, t0:t1, :], src[:, t0:t1, :], (t1 - t0) * C)
+            src = x_bytes[i // HI, i % HI].rearrange("(p t) c -> p t c", t=PACK)
+            load(("x", i, t0), x_raw[i][:, t0:t1, :], src[:, t0:t1, :], (t1 - t0) * C)
             for t in range(t0, t1):
                 arrived["x", i, t] = arrived["x", i, t0]
 
-        load_dl(0)
+        load_dl(0, 0)
+        load_dl(0, 1)
         load_x(0, 0, 1)
-        load_dl(1)
-        load_x(0, 1, 4)
+        load_dl(1, 0)
+        load_dl(1, 1)
+        load_x(0, 1, PACK)
         for q in range(4):
-            rows = slice(32 * q, 32 * q + 4)
             nc.sync.dma_start(
-                out=w_planes[rows, 0 : G * O].bitcast(I32).rearrange("q (g n) -> q g n", g=G),
+                out=w_scales[32 * q : 32 * q + 4, 0 : G * O].bitcast(I32).rearrange("q (g n) -> q g n", g=G),
                 in_=wc_scales[:, 4 * q : 4 * q + 4, :].bitcast(I32).rearrange("g q n -> q g n"),
             )
         for q in range(4):
-            rows = slice(32 * q, 32 * q + 4)
             nc.sync.dma_start(
-                out=w_planes[rows, G * O :].bitcast(I32),
+                out=w_scales[32 * q : 32 * q + 4, G * O :].bitcast(I32),
                 in_=ring_scales[0, 4 * q : 4 * q + 4, :].bitcast(I32),
             )
         load("wc", wc[:].bitcast(I32), wc_words.bitcast(I32).rearrange("g p n -> p g n"), 2 * G * O)
-        load_x(1, 0, 4)
-        load("ray", ray_raw[:], ray.rearrange("(c p) w -> p c w", p=P), 2 * NC * W)
+        load_x(1, 0, PACK)
+        load("ray", ray_raw[:], ray.rearrange("(c p) w -> p c w", p=P), 2 * CHUNKS * W)
         load("ring", ring[:].bitcast(I32), ring_words[0].bitcast(I32), 2 * CELLS)
         for i in range(2, B * HI):
-            load_x(i, 0, 4)
+            load_x(i, 0, PACK)
 
         tasks = []
 
         def task(key, engine, work, due, after, call, *holds):
             tasks.append((key, engine, work, due, after, call, holds))
 
-        def words(tile_view, pattern):
-            return tile_view.rearrange(pattern).bitcast(F32)
+        def as_words(view, pattern):
+            return view.rearrange(pattern).bitcast(F32)
 
         def turn_words(rows, dst):
             for u in range(2):
                 nc.tensor.transpose(dst[:, u, :], rows[:, u::2], ident[:])
 
-        banks = {"turns": S["bt"], "sums": 8 - S["bt"], "rows": 4, "wide": 4, "groups": 5, "codes": 5, "halves": 2}
-
-        scale = hold("scale", [C], F32)
-        gd512 = hold("gd512", [ND], F32)
-        gd4f = hold("gd4f", [T], F32)
-        gwf = hold("gwf", [T], F32)
-        gwn = hold("gwn", [T], F32)
+        scale_rows = hold("scale_rows", [C], F32)
+        gd_rows = hold("gd_rows", [ND], F32)
+        gd_cols = hold("gd_cols", [PACK], F32)
+        gw_cols = hold("gw_cols", [PACK], F32)
+        gw_mean = hold("gw_mean", [PACK], F32)
         spread = {}
 
         def spread_turn(name, cols):
-            xt = ps_t.tile([P, T, P], F32, name="xt")
-            for t in range(T):
-                nc.tensor.transpose(xt[:, t, :], cols[:, t : t + 1].to_broadcast([P, P]), ident[:])
-            spread[name] = xt
+            bank = psum_turned.tile([P, PACK, P], F32, name="bank")
+            for t in range(PACK):
+                nc.tensor.transpose(bank[:, t, :], cols[:, t : t + 1].to_broadcast([P, P]), ident[:])
+            spread[name] = bank
 
         def spread_copy(name, dst):
-            nc.scalar.copy(out=dst.rearrange("p (n t) -> p n t", t=T), in_=spread[name][:].rearrange("p t n -> p n t"))
+            nc.scalar.copy(out=dst.rearrange("p (n t) -> p n t", t=PACK), in_=spread[name][:].rearrange("p t n -> p n t"))
 
-        def small_vectors():
-            nc.vector.tensor_scalar(out=gd4f[:], in0=gd4[:], scalar1=float(ND), scalar2=None, op0=ALU.mult)
-            nc.vector.tensor_copy(out=gwf[:], in_=gw4[:])
-            nc.vector.tensor_scalar(out=gwn[:], in0=gw4[:], scalar1=-1.0 / O, scalar2=None, op0=ALU.mult)
+        def gain_columns():
+            nc.gpsimd.tensor_scalar(out=gd_cols[:], in0=gd_raw[:], scalar1=float(ND), scalar2=None, op0=ALU.mult)
+            nc.gpsimd.tensor_copy(out=gw_cols[:], in_=gw_raw[:])
+            nc.gpsimd.tensor_scalar(out=gw_mean[:], in0=gw_raw[:], scalar1=-1.0 / O, scalar2=None, op0=ALU.mult)
 
-        arrived["small"] = S["dlat"] + 300
-        task("small_v", "V", 60, 0, ["small"], small_vectors)
-        for j in range(G):
-            task(("st", j), "P", S["pw"], -2, ["small"], lambda j=j: spread_turn(j, scol[:, j, :]), ("turns", ("sc", j)))
-            task(("sc", j), "S", 512, -2, [("st", j)], lambda j=j: spread_copy(j, scale[:, 512 * j : 512 * (j + 1)]))
-        task("gt", "P", S["pw"], -1, ["small_v"], lambda: spread_turn("gd", gd4f), ("turns", "gc"))
-        task("gc", "S", 512, -1, ["gt"], lambda: spread_copy("gd", gd512[:]))
+        task("gain columns", "gpsimd", 500, 0, ["gains"], gain_columns)
+        for g in range(G):
+            task(
+                ("spread turn", g), "tensor", TENSOR_RUN, -2, ["scales"],
+                lambda g=g: spread_turn(g, scales[:, g, :]),
+                ("turned", ("scale rows", g)),
+            )
+            task(
+                ("scale rows", g), "scalar", 512, -2, [("spread turn", g)],
+                lambda g=g: spread_copy(g, scale_rows[:, K_PASS * g : K_PASS * (g + 1)]),
+            )
+        task(
+            "gd turn", "tensor", TENSOR_RUN, -1, ["gain columns"],
+            lambda: spread_turn("gd", gd_cols), ("turned", "gd rows"),
+        )
+        task("gd rows", "scalar", 512, -1, ["gd turn"], lambda: spread_copy("gd", gd_rows[:]))
 
-        m1 = hold_each("m1_", B, [T, ND // 2], BF16)
-        m2 = hold_each("m2_", B, [T, ND // 4], BF16)
-        mx = hold_each("mx", B, [T], F32)
-        negmax = hold_each("negmax", B, [T], F32)
-        esum = hold_each("esum", B, [T], F32)
-        rsum = hold_each("rsum", B, [T], F32)
-        e_t = hold_each("e", B, [T, ND], F32)
-        d_t = hold_each("d", B, [T, ND], BF16)
-        dg = hold_each("dg", B, [T, P, T], BF16)
-        d_codes = hold_each("dcodes", B, [W], U32)
-        d_planes = hold_each("dplanes", B, [W], U8)
+        max_256 = hold_each("max_256_", B, [PACK, ND // 2], BF16)
+        max_128 = hold_each("max_128_", B, [PACK, ND // 4], BF16)
+        row_max = hold_each("row_max", B, [PACK], F32)
+        minus_max = hold_each("minus_max", B, [PACK], F32)
+        exp_sum = hold_each("exp_sum", B, [PACK], F32)
+        inverse = hold_each("inverse", B, [PACK], F32)
+        exps = hold_each("exps", B, [PACK, ND], F32)
+        d_rows = hold_each("d_rows", B, [PACK, ND], BF16)
+        d_packed = hold_each("d_packed", B, [PACK, P, PACK], BF16)
+        d_codes = hold_each("d_codes", B, [W], U32)
+        d_scales = hold_each("d_scales", B, [W], U8)
         turned = {}
 
-        def d_max_1(b):
-            nc.vector.tensor_max(out=m1[b][:], in0=dls[b][:, :, 0 : ND // 2], in1=dls[b][:, :, ND // 2 :])
+        def max_to_256(b, half):
+            ts = slice(2 * half, 2 * half + 2)
+            nc.vector.tensor_max(
+                out=max_256[b][:, ts, :], in0=dl_raw[b][:, ts, 0 : ND // 2], in1=dl_raw[b][:, ts, ND // 2 :]
+            )
 
-        def d_max_2(b):
-            nc.vector.tensor_max(out=m2[b][:], in0=m1[b][:, :, 0 : ND // 4], in1=m1[b][:, :, ND // 4 :])
+        def max_to_128(b):
+            nc.vector.tensor_max(out=max_128[b][:], in0=max_256[b][:, :, 0 : ND // 4], in1=max_256[b][:, :, ND // 4 :])
 
-        def d_max_3(b):
-            nc.vector.reduce_max(out=mx[b][:], in_=m2[b][:], axis=AXIS.X)
+        def max_to_1(b):
+            nc.vector.reduce_max(out=row_max[b][:], in_=max_128[b][:], axis=mybir.AxisListType.X)
 
-        def d_max_4(b):
-            nc.vector.tensor_scalar(out=negmax[b][:], in0=mx[b][:], scalar1=-1.0, scalar2=None, op0=ALU.mult)
+        def negate_max(b):
+            nc.vector.tensor_scalar(out=minus_max[b][:], in0=row_max[b][:], scalar1=-1.0, scalar2=None, op0=ALU.mult)
 
-        def d_exp(b, t):
+        def exponentials(b, t):
             nc.scalar.activation(
-                out=e_t[b][:, t, :], in_=dls[b][:, t, :], func=ACT.Exp, bias=negmax[b][:, t : t + 1], accum_out=esum[b][:, t : t + 1]
+                out=exps[b][:, t, :], in_=dl_raw[b][:, t, :], func=ACT.Exp,
+                bias=minus_max[b][:, t : t + 1], accum_out=exp_sum[b][:, t : t + 1],
             )
 
-        def d_recip(b):
-            nc.vector.reciprocal(out=rsum[b][:], in_=esum[b][:])
+        def invert(b):
+            nc.vector.reciprocal(out=inverse[b][:], in_=exp_sum[b][:])
 
-        def d_mul(b, t):
+        def depth(b, t):
             nc.vector.scalar_tensor_tensor(
-                out=d_t[b][:, t, :], in0=e_t[b][:, t, :], scalar=rsum[b][:, t : t + 1], in1=gd512[:], op0=ALU.mult, op1=ALU.mult
+                out=d_rows[b][:, t, :], in0=exps[b][:, t, :], scalar=inverse[b][:, t : t + 1], in1=gd_rows[:],
+                op0=ALU.mult, op1=ALU.mult,
             )
 
-        def turn_pair(key, rows_of):
-            xt = ps_t.tile([P, 2, 2, P], F32, name="xt")
+        def turn_two(key, words_of):
+            bank = psum_turned.tile([P, 2, 2, P], F32, name="bank")
             for j in range(2):
-                turn_words(rows_of(j), xt[:, j])
-            turned[key] = xt
+                turn_words(words_of(j), bank[:, j])
+            turned[key] = bank
 
-        def untangle(key, dst):
+        def pack_two(key, dst):
             nc.scalar.copy(
-                out=words(dst, "p j n k -> p (j n k)").rearrange("p (j n u) -> p j n u", j=2, u=2),
+                out=as_words(dst, "p j n k -> p (j n k)").rearrange("p (j n u) -> p j n u", j=2, u=2),
                 in_=turned[key][:].rearrange("p j u n -> p j n u"),
             )
 
-        def d_quant(b):
+        def turn_depth(b, half):
+            turn_two(
+                ("d", b, half),
+                lambda j: as_words(d_rows[b][:, 2 * half + j : 2 * half + j + 1, :], "p t n -> p (t n)"),
+            )
+
+        def quantise_depth(b):
             nc.vector.quantize_mx(
-                out=d_codes[b][:].bitcast(FP8X4), scales=d_planes[b][:], in_=dg[b][:].rearrange("p t w k -> p (t w k)")
+                out=d_codes[b][:].bitcast(FP8X4), scales=d_scales[b][:],
+                in_=d_packed[b][:].rearrange("p t w k -> p (t w k)"),
             )
 
         for b in range(B):
-            due = S["d%d" % b]
-            task(("dm", b, 1), "V", 512, -8 + b, [("dl", b)], lambda b=b: d_max_1(b))
-            task(("dm", b, 2), "V", 256, -7 + b, [("dm", b, 1)], lambda b=b: d_max_2(b))
-            task(("dm", b, 3), "V", 512, -6 + b, [("dm", b, 2)], lambda b=b: d_max_3(b))
-            task(("dm", b, 4), "V", 10, -5 + b, [("dm", b, 3)], lambda b=b: d_max_4(b))
-            for t in range(T):
-                task(("de", b, t), "S", 560, S["e%d" % b], [("dm", b, 4)], lambda b=b, t=t: d_exp(b, t))
-            task(("dr", b), "V", 40, due, [("de", b, t) for t in range(T)], lambda b=b: d_recip(b))
-            for t in range(T):
-                task(("du", b, t), "V", 512, due + S["mst"] * t, [("dr", b), "gc"], lambda b=b, t=t: d_mul(b, t))
-            for h in range(2):
+            due = DUE["depth"][b]
+            for half in range(2):
+                task(("max 256", b, half), "vector", 256, b - 8, [("dl", b, half)], lambda b=b, half=half: max_to_256(b, half))
+            task(("max 128", b), "vector", 256, b - 7, [("max 256", b, 0), ("max 256", b, 1)], lambda b=b: max_to_128(b))
+            task(("max 1", b), "vector", 512, b - 6, [("max 128", b)], lambda b=b: max_to_1(b))
+            task(("minus max", b), "vector", 10, b - 5, [("max 1", b)], lambda b=b: negate_max(b))
+            for t in range(PACK):
+                task(("exp", b, t), "scalar", 560, DUE["exp"][b], [("minus max", b)], lambda b=b, t=t: exponentials(b, t))
+            task(("inverse", b), "vector", 40, due, [("exp", b, t) for t in range(PACK)], lambda b=b: invert(b))
+            for t in range(PACK):
                 task(
-                    ("dt", b, h), "P", S["pw"], due, [("du", b, 2 * h), ("du", b, 2 * h + 1)],
-                    lambda b=b, h=h: turn_pair(("d", b, h), lambda j: words(d_t[b][:, 2 * h + j : 2 * h + j + 1, :], "p t n -> p (t n)")),
-                    ("turns", ("dc", b, h)),
+                    ("depth", b, t), "vector", 512, due + DUE["depth step"] * t, [("inverse", b), "gd rows"],
+                    lambda b=b, t=t: depth(b, t),
                 )
-                task(("dc", b, h), "S", 512, due, [("dt", b, h)], lambda b=b, h=h: untangle(("d", b, h), dg[b][:, 2 * h : 2 * h + 2, :, :]))
-            task(("dq", b), "V", 512, due + 2, [("dc", b, 0), ("dc", b, 1)], lambda b=b: d_quant(b))
+            for half in range(2):
+                task(
+                    ("d turn", b, half), "tensor", TENSOR_RUN, due, [("depth", b, 2 * half), ("depth", b, 2 * half + 1)],
+                    lambda b=b, half=half: turn_depth(b, half), ("turned", ("d packed", b, half)),
+                )
+                task(
+                    ("d packed", b, half), "scalar", 512, due, [("d turn", b, half)],
+                    lambda b=b, half=half: pack_two(("d", b, half), d_packed[b][:, 2 * half : 2 * half + 2, :, :]),
+                )
+            task(("d codes", b), "vector", 512, due + 2, [("d packed", b, 0), ("d packed", b, 1)], lambda b=b: quantise_depth(b))
 
-        ray_t = hold("ray_t", [NC, P, T], BF16)
-        tmg = [hold("tmg", [NC, P, T], BF16)] * B
-        tm_codes = hold_each("tmcodes", B, [CELLS], U32)
-        tm_planes = hold_each("tmplanes", B, [CELLS], U8)
-        rds = {}
+        ray_packed = hold("ray_packed", [CHUNKS, P, PACK], BF16)
+        tm_packed = [hold("tm_packed", [CHUNKS, P, PACK], BF16)] * B
+        tm_codes = hold_each("tm_codes", B, [CELLS], U32)
+        tm_scales = hold_each("tm_scales", B, [CELLS], U8)
+        rd = {}
+
+        def turn_ray(i):
+            turn_two(("ray", i), lambda j: as_words(ray_raw[:, 2 * i + j : 2 * i + j + 1, :], "p c w -> p (c w)"))
 
         def transport(b, c):
-            rd = ps_y.tile([P, T, P], F32, name="acc")
-            for t in range(T):
+            bank = psum_sums.tile([P, PACK, P], F32, name="sums")
+            for t in range(PACK):
                 nc.tensor.matmul_mx(
-                    out=rd[:, t, :],
+                    out=bank[:, t, :],
                     lhsT=d_codes[b][:, P * t : P * (t + 1)].bitcast(FP8X4),
-                    lhsT_scale=d_planes[b][:, P * t : P * (t + 1)],
+                    lhsT_scale=d_scales[b][:, P * t : P * (t + 1)],
                     rhs=ring[:, 2 * P * c : 2 * P * (c + 1)].bitcast(FP4X4),
-                    rhs_scale=w_planes[:, G * O + P * c : G * O + P * (c + 1)],
+                    rhs_scale=w_scales[:, G * O + P * c : G * O + P * (c + 1)],
                     start=True,
                     stop=True,
                 )
-            rds[b, c] = rd
+            rd[b, c] = bank
 
         def weigh(b, c):
             nc.vector.tensor_tensor(
-                out=tmg[b][:, c, :, :], in0=rds[b, c][:].rearrange("p t n -> p n t"), in1=ray_t[:, c, :, :], op=ALU.mult
+                out=tm_packed[b][:, c, :, :], in0=rd[b, c][:].rearrange("p t n -> p n t"), in1=ray_packed[:, c, :, :],
+                op=ALU.mult,
             )
 
-        def tm_quant(b, c, n):
+        def quantise_transport(b, c):
             nc.vector.quantize_mx(
-                out=tm_codes[b][:, P * c : P * (c + n)].bitcast(FP8X4),
-                scales=tm_planes[b][:, P * c : P * (c + n)],
-                in_=tmg[b][:, c : c + n, :, :].rearrange("p c n k -> p (c n k)"),
+                out=tm_codes[b][:, P * c : P * (c + 2)].bitcast(FP8X4),
+                scales=tm_scales[b][:, P * c : P * (c + 2)],
+                in_=tm_packed[b][:, c : c + 2, :, :].rearrange("p c n k -> p (c n k)"),
             )
 
-        for i in range(NC // 2):
-            due = S["ray"] + S["rayst"] * i
+        for i in range(CHUNKS // 2):
+            due = DUE["ray"] + DUE["ray step"] * i
             task(
-                ("rt", i), "P", S["pw"], due, ["ray"],
-                lambda i=i: turn_pair(("ray", i), lambda j: words(ray_raw[:, 2 * i + j : 2 * i + j + 1, :], "p c w -> p (c w)")),
-                ("turns", ("rc", i)),
+                ("ray turn", i), "tensor", TENSOR_RUN, due, ["ray"], lambda i=i: turn_ray(i),
+                ("turned", ("ray packed", i)),
             )
-            task(("rc", i), "S", 512, due, [("rt", i)], lambda i=i: untangle(("ray", i), ray_t[:, 2 * i : 2 * i + 2, :, :]))
+            task(
+                ("ray packed", i), "scalar", 512, due, [("ray turn", i)],
+                lambda i=i: pack_two(("ray", i), ray_packed[:, 2 * i : 2 * i + 2, :, :]),
+            )
         for b in range(B):
-            for c in range(NC):
-                due = S["w%d" % b] + S["wst%d" % b] * c
-                task(("tr", b, c), "P", S["pw"] // 2, due - 1, [("dq", b), "ring"], lambda b=b, c=c: transport(b, c), ("sums", ("we", b, c)))
-                task(("we", b, c), "V", 512, due, [("tr", b, c), ("rc", c // 2)] + ([("tq", b - 1, c // 2)] if b else []), lambda b=b, c=c: weigh(b, c))
+            for c in range(CHUNKS):
+                due = DUE["transport"][b] + DUE["transport step"][b] * c
+                if b == 0 and c >= LATE_CHUNK:
+                    due = DUE["late transport"] + c
+                task(
+                    ("rd", b, c), "tensor", TENSOR_RUN // 2, due - 1, [("d codes", b), "ring"],
+                    lambda b=b, c=c: transport(b, c), ("sums", ("tm", b, c)),
+                )
+                after = [("rd", b, c), ("ray packed", c // 2)]
+                if b:
+                    after = after + [("tm codes", b - 1, c // 2)]
+                task(("tm", b, c), "vector", 512, due, after, lambda b=b, c=c: weigh(b, c))
                 if c % 2 == 1:
-                    task(("tq", b, c // 2), "V", 256, due + S["tqd"], [("we", b, c - 1), ("we", b, c)], lambda b=b, c=c: tm_quant(b, c - 1, 2))
+                    task(
+                        ("tm codes", b, c // 2), "vector", 256, due + DUE["transport codes"],
+                        [("tm", b, c - 1), ("tm", b, c)], lambda b=b, c=c: quantise_transport(b, c - 1),
+                    )
 
-        m_t = hold_each("m", B, [T, O], F32)
-        msum = hold_each("msum", B, [T], F32)
-        bias = hold_each("bias", B, [T], F32)
-        ctxp = [hold("ctxp", [2, O, 2], BF16)] * B
-        ctxg = [hold("ctxg", [O, T], BF16)] * B
-        c_codes = hold_each("ccodes", B, [O], U32)
-        c_planes = hold_each("cplanes", B, [O], U8)
-        xs, xg, x_codes, x_planes, halves, y_ps, accs = {}, {}, {}, {}, {}, {}, {}
+        m = hold_each("m", B, [PACK, O], F32)
+        m_sum = hold_each("m_sum", B, [PACK], F32)
+        offset = hold_each("offset", B, [PACK], F32)
+        ctx_halves = [hold("ctx_halves", [2, O, 2], BF16)] * B
+        ctx_packed = [hold("ctx_packed", [O, PACK], BF16)] * B
+        ctx_codes = hold_each("ctx_codes", B, [O], U32)
+        ctx_scales = hold_each("ctx_scales", B, [O], U8)
+        x_rows, x_packed, x_codes, x_scales, x_halves, y, result_bank = {}, {}, {}, {}, {}, {}, {}
 
-        def group_tiles(s):
-            xg[s] = flow.tile([P, G, 2, P, T], BF16, name="xg_s", align_bytes=64, bufs=banks["groups"])
-            x_codes[s] = flow.tile([P, G, 2, P], U32, name="xcodes_s", align_bytes=64, bufs=banks["codes"])
-            x_planes[s] = flow.tile([P, G, 2, P], U8, name="xplanes_s", align_bytes=64, bufs=banks["codes"])
+        def pair_tiles(s):
+            x_packed[s] = flow.tile([P, G, 2, P, PACK], BF16, name="x_packed_s", align_bytes=64, bufs=SLOTS["pairs"])
+            x_codes[s] = flow.tile([P, G, 2, P], U32, name="x_codes_s", align_bytes=64, bufs=SLOTS["codes"])
+            x_scales[s] = flow.tile([P, G, 2, P], U8, name="x_scales_s", align_bytes=64, bufs=SLOTS["codes"])
 
-        def scale_rows(q):
+        def scale_unit(q):
             if q % 2 == 0:
-                group_tiles(q // 2)
-            xs[q] = flow.tile([P, C], BF16, name="xs_q", align_bytes=64, bufs=banks["rows"])
-            nc.vector.tensor_tensor(out=xs[q][:], in0=raw[q // T][:, q % T, :].bitcast(F8), in1=scale[:], op=ALU.mult)
-
-        def widen(q):
-            xs[q] = flow.tile([P, C], BF16, name="xw_q", align_bytes=64, bufs=banks["wide"])
-            nc.scalar.copy(out=xs[q][:], in_=raw[q // T][:, q % T, :].bitcast(F8))
-
-        def turn(q):
-            turn_pair(("x", q), lambda g: xs[q][:, 512 * g : 512 * (g + 1)].bitcast(F32))
-
-        def turn_copy(q):
-            s, k = divmod(q, 2)
-            nc.scalar.copy(
-                out=xg[s][:].rearrange("p g k r t -> p (g k r t)").bitcast(F32).rearrange("p (g k r u) -> p g k r u", g=G, k=2, u=2)[:, :, k],
-                in_=turned["x", q][:].rearrange("p g u r -> p g r u"),
+                pair_tiles(q // 2)
+            x_rows[q] = flow.tile([P, C], BF16, name="x_rows_q", align_bytes=64, bufs=SLOTS["rows"])
+            nc.vector.tensor_tensor(
+                out=x_rows[q][:], in0=x_raw[q // PACK][:, q % PACK, :].bitcast(F8), in1=scale_rows[:], op=ALU.mult
             )
 
-        def turn_pass(s, g):
+        def turn_unit(q):
+            turn_two(("x", q), lambda g: x_rows[q][:, K_PASS * g : K_PASS * (g + 1)].bitcast(F32))
+
+        def pack_unit(q):
+            s, k = divmod(q, 2)
+            words = as_words(x_packed[s][:], "p g k r t -> p (g k r t)").rearrange("p (g k r u) -> p g k r u", g=G, k=2, u=2)
+            nc.scalar.copy(out=words[:, :, k], in_=turned["x", q][:].rearrange("p g u r -> p g r u"))
+
+        def widen_unit(q):
+            x_rows[q] = flow.tile([P, C], BF16, name="x_wide_q", align_bytes=64, bufs=SLOTS["wide"])
+            nc.scalar.copy(out=x_rows[q][:], in_=x_raw[q // PACK][:, q % PACK, :].bitcast(F8))
+
+        def turn_pair(s, g):
             if g == 0:
-                halves[s] = flow.tile([P, G, 2, 2 * P, 2], BF16, name="halves_s", align_bytes=64, bufs=banks["halves"])
-            turn_pair(("h", s, g), lambda k: xs[2 * s + k][:, 512 * g : 512 * (g + 1)].bitcast(F32))
+                x_halves[s] = flow.tile([P, G, 2, 2 * P, 2], BF16, name="x_halves_s", align_bytes=64, bufs=SLOTS["halves"])
+            turn_two(("pair", s, g), lambda k: x_rows[2 * s + k][:, K_PASS * g : K_PASS * (g + 1)].bitcast(F32))
 
         def scale_turned(s, g, u):
-            values = turned["h", s, g][:].rearrange("p k u r -> p (k u r)").bitcast(BF16).rearrange("p (k u r e) -> p k u r e", k=2, u=2, e=2)
+            bank = turned["pair", s, g][:].rearrange("p k u r -> p (k u r)").bitcast(BF16)
+            values = bank.rearrange("p (k u r e) -> p k u r e", k=2, u=2, e=2)
             for e in range(2):
                 nc.scalar.activation(
-                    out=halves[s][:, g, u, :, e].rearrange("p (k r) -> p k r", k=2),
+                    out=x_halves[s][:, g, u, :, e].rearrange("p (k r) -> p k r", k=2),
                     in_=values[:, :, u, :, e],
                     func=ACT.Copy,
-                    scale=scol[:, g, 2 * u + e : 2 * u + e + 1],
+                    scale=scales[:, g, 2 * u + e : 2 * u + e + 1],
                 )
 
-        def weave(s):
-            group_tiles(s)
-            nc.vector.tensor_copy(
-                out=words(xg[s][:], "p g k r t -> p (g k r t)").rearrange("p (g c u) -> p g c u", g=G, u=2),
-                in_=words(halves[s][:], "p g u c e -> p (g u c e)").rearrange("p (g u c) -> p g c u", g=G, u=2),
+        def weave_pair(s):
+            pair_tiles(s)
+            copy = nc.scalar.copy if s in SCALAR_WEAVES else nc.vector.tensor_copy
+            copy(
+                out=as_words(x_packed[s][:], "p g k r t -> p (g k r t)").rearrange("p (g c u) -> p g c u", g=G, u=2),
+                in_=as_words(x_halves[s][:], "p g u c e -> p (g u c e)").rearrange("p (g u c) -> p g c u", g=G, u=2),
             )
 
-        def quant(s):
+        def quantise_pair(s):
             nc.vector.quantize_mx(
                 out=x_codes[s][:].rearrange("p g k r -> p (g k r)").bitcast(FP8X4),
-                scales=x_planes[s][:].rearrange("p g k r -> p (g k r)"),
-                in_=xg[s][:].rearrange("p g k r t -> p (g k r t)"),
+                scales=x_scales[s][:].rearrange("p g k r -> p (g k r)"),
+                in_=x_packed[s][:].rearrange("p g k r t -> p (g k r t)"),
             )
 
         def project(q):
             s, k = divmod(q, 2)
-            y_ps[q] = ps_y.tile([P, O], F32, name="acc")
+            y[q] = psum_sums.tile([P, O], F32, name="sums")
             for g in range(G):
                 nc.tensor.matmul_mx(
-                    out=y_ps[q][:],
+                    out=y[q][:],
                     lhsT=x_codes[s][:, g, k, :].bitcast(FP8X4),
-                    lhsT_scale=x_planes[s][:, g, k, :],
+                    lhsT_scale=x_scales[s][:, g, k, :],
                     rhs=wc[:, g, :].bitcast(FP4X4),
-                    rhs_scale=w_planes[:, O * g : O * (g + 1)],
+                    rhs_scale=w_scales[:, O * g : O * (g + 1)],
                     start=(g == 0),
                     stop=(g == G - 1),
                 )
 
         def height_max(q):
-            i, t = divmod(q, T)
+            i, t = divmod(q, PACK)
             b, h = divmod(i, HI)
-            m = m_t[b][:, t, :]
+            running = m[b][:, t, :]
             if h == 0:
-                nc.scalar.copy(out=m, in_=y_ps[q][:])
+                nc.scalar.copy(out=running, in_=y[q][:])
             elif h < HI - 1:
-                nc.vector.tensor_max(out=m, in0=y_ps[q][:], in1=m)
+                nc.vector.tensor_max(out=running, in0=y[q][:], in1=running)
             else:
                 nc.vector.scalar_tensor_tensor(
-                    out=m, in0=y_ps[q][:], scalar=1.0, in1=m, op0=ALU.mult, op1=ALU.max, accum_out=msum[b][:, t : t + 1]
+                    out=running, in0=y[q][:], scalar=1.0, in1=running, op0=ALU.mult, op1=ALU.max,
+                    accum_out=m_sum[b][:, t : t + 1],
                 )
 
+        def centring_offset(b, t):
+            nc.gpsimd.tensor_scalar(
+                out=offset[b][:, t : t + 1], in0=m_sum[b][:, t : t + 1], scalar1=gw_mean[:, t : t + 1], scalar2=None,
+                op0=ALU.mult,
+            )
+
         def centre(b, t):
-            nc.scalar.activation(out=bias[b][:, t : t + 1], in_=msum[b][:, t : t + 1], func=ACT.Copy, scale=gwn[:, t : t + 1])
             nc.scalar.activation(
-                out=ctxp[b][:, t // 2, :, t % 2], in_=m_t[b][:, t, :], func=ACT.Identity, scale=gwf[:, t : t + 1], bias=bias[b][:, t : t + 1]
+                out=ctx_halves[b][:, t // 2, :, t % 2], in_=m[b][:, t, :], func=ACT.Identity,
+                scale=gw_cols[:, t : t + 1], bias=offset[b][:, t : t + 1],
             )
 
-        def ctx_weave(b):
-            nc.vector.tensor_copy(
-                out=words(ctxg[b][:], "p o t -> p (o t)").rearrange("p (o u) -> p o u", u=2),
-                in_=words(ctxp[b][:], "p u o e -> p (u o e)").rearrange("p (u o) -> p o u", u=2),
+        def weave_context(b):
+            copy = nc.scalar.copy if b in SCALAR_CTX_WEAVES else nc.vector.tensor_copy
+            copy(
+                out=as_words(ctx_packed[b][:], "p o t -> p (o t)").rearrange("p (o u) -> p o u", u=2),
+                in_=as_words(ctx_halves[b][:], "p u o e -> p (u o e)").rearrange("p (u o) -> p o u", u=2),
             )
 
-        def ctx_quant(b):
+        def quantise_context(b):
             nc.vector.quantize_mx(
-                out=c_codes[b][:].bitcast(FP8X4), scales=c_planes[b][:], in_=ctxg[b][:].rearrange("p o t -> p (o t)")
+                out=ctx_codes[b][:].bitcast(FP8X4), scales=ctx_scales[b][:],
+                in_=ctx_packed[b][:].rearrange("p o t -> p (o t)"),
             )
 
         def result(b, c):
-            acc = ps_y.tile([P, O], F32, name="acc")
+            bank = psum_sums.tile([P, O], F32, name="sums")
             nc.tensor.matmul_mx(
-                out=acc[:],
+                out=bank[:],
                 lhsT=tm_codes[b][:, P * c : P * (c + 1)].bitcast(FP8X4),
-                lhsT_scale=tm_planes[b][:, P * c : P * (c + 1)],
-                rhs=c_codes[b][:].bitcast(FP8X4),
-                rhs_scale=c_planes[b][:],
+                lhsT_scale=tm_scales[b][:, P * c : P * (c + 1)],
+                rhs=ctx_codes[b][:].bitcast(FP8X4),
+                rhs_scale=ctx_scales[b][:],
                 start=True,
                 stop=True,
             )
-            accs[b, c] = acc
+            result_bank[b, c] = bank
 
-        def emit(b, c, engine):
-            res = stores.tile([P, O], F32, name="res", align_bytes=64)
-            if engine == "V":
-                nc.vector.tensor_copy(out=res[:], in_=accs[b, c][:])
-            else:
-                nc.scalar.copy(out=res[:], in_=accs[b, c][:])
-            nc.sync.dma_start(out=out[b, P * c : P * (c + 1), :], in_=res[:])
+        def store(b, c, engine):
+            rows = stores.tile([P, O], F32, name="rows", align_bytes=64)
+            copy = nc.vector.tensor_copy if engine == "vector" else nc.scalar.copy
+            copy(out=rows[:], in_=result_bank[b, c][:])
+            nc.sync.dma_start(out=out[b, P * c : P * (c + 1), :], in_=rows[:])
 
         for s in range(N_UNITS // 2):
             pair = (2 * s, 2 * s + 1)
-            if s in S["HP"]:
+            pair_holds = [("pairs", ("x codes", s)), ("codes", ("y", 2 * s + 1))]
+            if s in SCALAR_PAIRS:
                 for q in pair:
-                    task(("tt", q), "S", 1024, q - S["wid"], [("x", q // T, q % T)], lambda q=q: widen(q), ("wide", ("tp", s, 1)))
-                for g in range(G):
-                    due = 2 * s - S["th"] + 2 * g
                     task(
-                        ("tp", s, g), "P", S["pw"], due, [("tt", q) for q in pair] + ([("tp", s, 0)] if g else []), lambda s=s, g=g: turn_pass(s, g),
-                        ("turns", ("ex", s, g, 1)), *([] if g else [("halves", ("wv", s))]),
+                        ("x rows", q), "scalar", 1024, q + DUE["widen"], [("x", q // PACK, q % PACK)],
+                        lambda q=q: widen_unit(q), ("wide", ("pair turn", s, 1)),
+                    )
+                for g in range(G):
+                    due = 2 * s + DUE["pair turn"] + 2 * g
+                    after = [("x rows", q) for q in pair]
+                    if g:
+                        after = after + [("pair turn", s, 0)]
+                    task(
+                        ("pair turn", s, g), "tensor", TENSOR_RUN, due, after, lambda s=s, g=g: turn_pair(s, g),
+                        ("turned", ("x halves", s, g, 1)), *([] if g else [("halves", ("weave", s))]),
                     )
                     for u in range(2):
-                        task(("ex", s, g, u), "S", 780, due + u, [("tp", s, g)], lambda s=s, g=g, u=u: scale_turned(s, g, u))
-                task(("wv", s), "V", 512, 2 * s, [("ex", s, g, u) for g in range(G) for u in range(2)], lambda s=s: weave(s), ("groups", ("qu", s)), ("codes", ("pr", 2 * s + 1)))
-                ready = [("wv", s)]
+                        task(
+                            ("x halves", s, g, u), "scalar", 780, due + u, [("pair turn", s, g)],
+                            lambda s=s, g=g, u=u: scale_turned(s, g, u),
+                        )
+                task(
+                    ("weave", s), "scalar" if s in SCALAR_WEAVES else "vector", 1024 if s in SCALAR_WEAVES else 512, 2 * s,
+                    [("x halves", s, g, u) for g in range(G) for u in range(2)], lambda s=s: weave_pair(s), *pair_holds,
+                )
+                packed = [("weave", s)]
             else:
                 for q in pair:
-                    task(("tt", q), "V", 1024, q, [("x", q // T, q % T), ("sc", 0), ("sc", 1)], lambda q=q: scale_rows(q), ("rows", ("tu", q)), *([] if q % 2 else [("groups", ("qu", s)), ("codes", ("pr", q + 1))]))
-                    task(("tu", q), "P", S["pw"], q, [("tt", q)], lambda q=q: turn(q), ("turns", ("cp", q)))
-                    task(("cp", q), "S", 512, q, [("tu", q)], lambda q=q: turn_copy(q))
-                ready = [("cp", q) for q in pair]
-            task(("qu", s), "V", 512, 2 * s + S["qd"], ready, lambda s=s: quant(s))
+                    first_unit = [("x rows", q - 1)] if q % 2 else []
+                    task(
+                        ("x rows", q), "vector", 1024, q,
+                        [("x", q // PACK, q % PACK), ("scale rows", 0), ("scale rows", 1)] + first_unit,
+                        lambda q=q: scale_unit(q), ("rows", ("x turn", q)), *([] if q % 2 else pair_holds),
+                    )
+                    task(
+                        ("x turn", q), "tensor", TENSOR_RUN, q, [("x rows", q)], lambda q=q: turn_unit(q),
+                        ("turned", ("x packed", q)),
+                    )
+                    task(("x packed", q), "scalar", 512, q, [("x turn", q)], lambda q=q: pack_unit(q))
+                packed = [("x packed", q) for q in pair]
+            task(("x codes", s), "vector", 512, 2 * s + DUE["quantise"], packed, lambda s=s: quantise_pair(s))
             for q in pair:
-                i, t = divmod(q, T)
-                b, h = divmod(i, HI)
-                task(("pr", q), "P", S["pw"], q + S["pd"], [("qu", s), "wc"], lambda q=q: project(q), ("sums", ("hm", q)))
-                engine = "S" if h == 0 else "V"
-                before = [("hm", q - T)] if h else []
-                task(("hm", q), engine, 512, q + S["hd"], [("pr", q)] + before, lambda q=q: height_max(q))
+                h = q // PACK % HI
+                first_unit = [("y", q - 1)] if q % 2 else []
+                task(
+                    ("y", q), "tensor", TENSOR_RUN, q + DUE["project"], [("x codes", s), "wc"] + first_unit,
+                    lambda q=q: project(q), ("sums", ("m", q)),
+                )
+                before = [("m", q - PACK)] if h else []
+                task(
+                    ("m", q), "vector" if h else "scalar", 512, q + DUE["height maximum"], [("y", q)] + before,
+                    lambda q=q: height_max(q),
+                )
         for b in range(B):
-            for t in range(T):
-                task(("ce", b, t), "S", 900, S["ce"] + 16 * b, [("hm", (b * HI + HI - 1) * T + t)] + ([("cw", b - 1)] if b else []), lambda b=b, t=t: centre(b, t))
-            task(("cw", b), "V", 512, S["cw"] + 13 * b, [("ce", b, t) for t in range(T)] + ([("cq", b - 1)] if b else []), lambda b=b: ctx_weave(b))
-            task(("cq", b), "V", 512, S["cw"] + 13 * b, [("cw", b)], lambda b=b: ctx_quant(b))
-            for c in range(NC):
-                engine = "V" if b == 1 and c >= S["ev"] and c % 2 == 1 else "S"
-                due = S["re"] + c * S["rest"] + 20 * b
-                task(("re", b, c), "P", S["pw"] // 2, due, [("cq", b), ("tq", b, c // 2)], lambda b=b, c=c: result(b, c), ("sums", ("em", b, c)))
-                task(("em", b, c), engine, 512, due, [("re", b, c)], lambda b=b, c=c, engine=engine: emit(b, c, engine))
+            halves_free = [("ctx weave", b - 1)] if b else []
+            packed_free = [("ctx codes", b - 1)] if b else []
+            for t in range(PACK):
+                task(
+                    ("offset", b, t), "gpsimd", 200, 0, [("m", (b * HI + HI - 1) * PACK + t), "gain columns"],
+                    lambda b=b, t=t: centring_offset(b, t),
+                )
+                task(
+                    ("ctx halves", b, t), "scalar", 780, DUE["centre"] + DUE["centre step"] * b,
+                    [("offset", b, t)] + halves_free, lambda b=b, t=t: centre(b, t),
+                )
+            due = DUE["context"] + DUE["context step"] * b
+            on_scalar = b in SCALAR_CTX_WEAVES
+            task(
+                ("ctx weave", b), "scalar" if on_scalar else "vector", 1024 if on_scalar else 512, due,
+                [("ctx halves", b, t) for t in range(PACK)] + packed_free, lambda b=b: weave_context(b),
+            )
+            task(("ctx codes", b), "vector", 512, due, [("ctx weave", b)], lambda b=b: quantise_context(b))
+            for c in range(CHUNKS):
+                engine = "vector" if b == B - 1 and c in VECTOR_RESULTS else "scalar"
+                due = DUE["result"] + DUE["result step"] * c + DUE["result batch step"] * b
+                task(
+                    ("result", b, c), "tensor", TENSOR_RUN // 2, due, [("ctx codes", b), ("tm codes", b, c // 2)],
+                    lambda b=b, c=c: result(b, c), ("sums", ("store", b, c)),
+                )
+                task(
+                    ("store", b, c), engine, 512, due, [("result", b, c)],
+                    lambda b=b, c=c, engine=engine: store(b, c, engine),
+                )
 
-        for call in list_order(tasks, banks, arrived):
+        for call in list_order(tasks, arrived):
             call()

from contextlib import ExitStack

import concourse.mybir as mybir
from concourse.masks import make_identity

F32 = mybir.dt.float32
BF16 = mybir.dt.bfloat16
I32 = mybir.dt.int32
U32 = mybir.dt.uint32
U8 = mybir.dt.uint8
F8 = mybir.dt.float8_e4m3fn
FP8X4 = mybir.dt.float8_e4m3fn_x4
FP4X4 = mybir.dt.float4_e2m1fn_x4
ALU = mybir.AluOpType
ACT = mybir.ActivationFunctionType

B, HI, W, C, ND, CELLS, O = 2, 4, 512, 1024, 512, 1024, 512
P = 128
PACK = 4
K_PASS = P * PACK
G = C // K_PASS
CHUNKS = CELLS // P
N_UNITS = B * HI * PACK
FLOPS = 2 * B * HI * W * C * O + 2 * B * CELLS * W * ND + 2 * B * CELLS * W * O

SCALAR_PAIRS = (8, 9, 11, 14)
SCALAR_WEAVES = (8, 14)
SCALAR_CTX_WEAVES = (1,)
VECTOR_RESULTS = (6, 7)

SLOTS = {"turned": 4, "sums": 4, "rows": 4, "wide": 4, "pairs": 5, "codes": 5, "halves": 2}

CALL = 60
HANDOFF = 540
SAME_ENGINE = 160
LOAD_START = 1600
TENSOR_RUN = 680

DUE = {
    "exp": (-100, -20.5),
    "depth": (-26, 23.5),
    "depth step": 6.5,
    "ray": 16.5,
    "ray step": 2,
    "transport": (-7, 153),
    "transport step": (4.75, 11),
    "late transport": 80,
    "transport codes": -30.5,
    "widen": 15.5,
    "pair turn": -9,
    "quantise": -6,
    "project": 4.5,
    "height maximum": 8,
    "centre": 22,
    "centre step": 16,
    "context": 10.5,
    "context step": 13,
    "result": 10.5,
    "result step": 12.5,
    "result batch step": 20,
}
LATE_CHUNK = 4


def list_order(tasks, arrived):
    done = {key: (time, "load") for key, time in arrived.items()}
    free = {"vector": 0, "scalar": 0, "tensor": 0, "gpsimd": 0}
    taken = {kind: [] for kind in SLOTS}
    lacking = {}
    users = {}
    open_tasks = []

    def usable(key, engine):
        time, maker = done[key]
        if maker == "load":
            return time
        return time + (SAME_ENGINE if maker == engine else HANDOFF)

    for task in tasks:
        missing = [k for k in task[4] if k not in done]
        lacking[task[0]] = len(missing)
        for k in missing:
            users.setdefault(k, []).append(task)
        if not missing:
            open_tasks.append((max([usable(k, task[1]) for k in task[4]]), task))
    order = []
    while open_tasks:
        best = None
        for item in open_tasks:
            ready, task = item
            ready = max(ready, free[task[1]])
            blocked = False
            for kind, last_use in task[6]:
                if len(taken[kind]) >= SLOTS[kind]:
                    previous = taken[kind][-SLOTS[kind]]
                    if previous in done:
                        ready = max(ready, usable(previous, task[1]))
                    else:
                        blocked = True
            if blocked:
                continue
            rank = (ready, task[3])
            if best is None or rank < best[0]:
                best = (rank, item)
        (ready, due), item = best
        open_tasks.remove(item)
        key, engine, work, due, after, call, holds = item[1]
        free[engine] = ready + work + CALL
        done[key] = (free[engine], engine)
        for kind, last_use in holds:
            taken[kind].append(last_use)
        for task in users.get(key, []):
            lacking[task[0]] -= 1
            if lacking[task[0]] == 0:
                open_tasks.append((max(usable(k, task[1]) for k in task[4]), task))
        order.append(call)
    assert len(order) == len(tasks)
    return order


def tile_matrixvtringraybev_w4_kernel(
    tc, x_bytes, x_scale, wc_words, wc_scales, gw, dl, gd, ring_words, ring_scales, ray, out
):
    nc = tc.nc
    with ExitStack() as ctx:
        keep = ctx.enter_context(tc.tile_pool(name="keep", bufs=1))
        flow = ctx.enter_context(tc.tile_pool(name="flow", bufs=4))
        stores = ctx.enter_context(tc.tile_pool(name="stores", bufs=8))
        psum_turned = ctx.enter_context(tc.psum_pool(name="psum_turned", bufs=SLOTS["turned"]))
        psum_sums = ctx.enter_context(tc.psum_pool(name="psum_sums", bufs=SLOTS["sums"]))
        ctx.enter_context(tc.manual_schedule())

        def hold(name, shape, dtype):
            return keep.tile([P] + shape, dtype, name=name, align_bytes=64)

        def hold_each(name, n, shape, dtype):
            return [keep.tile([P] + shape, dtype, name="%s%d" % (name, i), align_bytes=64) for i in range(n)]

        scales = hold("scales", [G, PACK], F32)
        nc.scalar.dma_start(out=scales[:], in_=x_scale.rearrange("a b c (g p t) -> p (a b c g) t", p=P, t=PACK))
        gd_raw = hold("gd_raw", [PACK], BF16)
        nc.scalar.dma_start(out=gd_raw[:], in_=gd.rearrange("(p t) -> p t", p=P))
        gw_raw = hold("gw_raw", [PACK], BF16)
        nc.scalar.dma_start(out=gw_raw[:], in_=gw.rearrange("(p t) -> p t", p=P))

        first = hold("first", [1], F32)
        first_out = hold("first_out", [1], F32)
        nc.vector.memset(first[:], 0.0)
        nc.scalar.activation(out=first_out[:], in_=first[:], func=ACT.Exp)

        ident = hold("ident", [P], F32)
        make_identity(nc, ident[:])
        w_scales = hold("w_scales", [G * O + CELLS], U8)
        nc.gpsimd.memset(w_scales[:].bitcast(I32), 0)

        dl_raw = hold_each("dl_raw", B, [PACK, ND], BF16)
        x_raw = hold_each("x_raw", B * HI, [PACK, C], U8)
        wc = hold("wc", [G, 2 * O], U8)
        ring = hold("ring", [2 * CELLS], U8)
        ray_raw = hold("ray_raw", [CHUNKS, W], BF16)
        arrived = {"scales": LOAD_START, "gains": LOAD_START + 800}
        loaded = [0]

        def load(key, dst, src, size):
            nc.sync.dma_start(out=dst, in_=src)
            loaded[0] += size
            arrived[key] = LOAD_START + loaded[0] // 4

        def load_dl(b, half):
            ts = slice(2 * half, 2 * half + 2)
            load(("dl", b, half), dl_raw[b][:, ts, :], dl[b].rearrange("(p t) n -> p t n", t=PACK)[:, ts, :], 4 * ND)

        def load_x(i, t0, t1):
            src = x_bytes[i // HI, i % HI].rearrange("(p t) c -> p t c", t=PACK)
            load(("x", i, t0), x_raw[i][:, t0:t1, :], src[:, t0:t1, :], (t1 - t0) * C)
            for t in range(t0, t1):
                arrived["x", i, t] = arrived["x", i, t0]

        load_dl(0, 0)
        load_dl(0, 1)
        load_x(0, 0, 1)
        load_dl(1, 0)
        load_dl(1, 1)
        load_x(0, 1, PACK)
        for q in range(4):
            nc.sync.dma_start(
                out=w_scales[32 * q : 32 * q + 4, 0 : G * O].bitcast(I32).rearrange("q (g n) -> q g n", g=G),
                in_=wc_scales[:, 4 * q : 4 * q + 4, :].bitcast(I32).rearrange("g q n -> q g n"),
            )
        for q in range(4):
            nc.sync.dma_start(
                out=w_scales[32 * q : 32 * q + 4, G * O :].bitcast(I32),
                in_=ring_scales[0, 4 * q : 4 * q + 4, :].bitcast(I32),
            )
        load("wc", wc[:].bitcast(I32), wc_words.bitcast(I32).rearrange("g p n -> p g n"), 2 * G * O)
        load_x(1, 0, PACK)
        load("ray", ray_raw[:], ray.rearrange("(c p) w -> p c w", p=P), 2 * CHUNKS * W)
        load("ring", ring[:].bitcast(I32), ring_words[0].bitcast(I32), 2 * CELLS)
        for i in range(2, B * HI):
            load_x(i, 0, PACK)

        tasks = []

        def task(key, engine, work, due, after, call, *holds):
            tasks.append((key, engine, work, due, after, call, holds))

        def as_words(view, pattern):
            return view.rearrange(pattern).bitcast(F32)

        def turn_words(rows, dst):
            for u in range(2):
                nc.tensor.transpose(dst[:, u, :], rows[:, u::2], ident[:])

        scale_rows = hold("scale_rows", [C], F32)
        gd_rows = hold("gd_rows", [ND], F32)
        gd_cols = hold("gd_cols", [PACK], F32)
        gw_cols = hold("gw_cols", [PACK], F32)
        gw_mean = hold("gw_mean", [PACK], F32)
        spread = {}

        def spread_turn(name, cols):
            bank = psum_turned.tile([P, PACK, P], F32, name="bank")
            for t in range(PACK):
                nc.tensor.transpose(bank[:, t, :], cols[:, t : t + 1].to_broadcast([P, P]), ident[:])
            spread[name] = bank

        def spread_copy(name, dst):
            nc.scalar.copy(out=dst.rearrange("p (n t) -> p n t", t=PACK), in_=spread[name][:].rearrange("p t n -> p n t"))

        def gain_columns():
            nc.gpsimd.tensor_scalar(out=gd_cols[:], in0=gd_raw[:], scalar1=float(ND), scalar2=None, op0=ALU.mult)
            nc.gpsimd.tensor_copy(out=gw_cols[:], in_=gw_raw[:])
            nc.gpsimd.tensor_scalar(out=gw_mean[:], in0=gw_raw[:], scalar1=-1.0 / O, scalar2=None, op0=ALU.mult)

        task("gain columns", "gpsimd", 500, 0, ["gains"], gain_columns)
        for g in range(G):
            task(
                ("spread turn", g), "tensor", TENSOR_RUN, -2, ["scales"],
                lambda g=g: spread_turn(g, scales[:, g, :]),
                ("turned", ("scale rows", g)),
            )
            task(
                ("scale rows", g), "scalar", 512, -2, [("spread turn", g)],
                lambda g=g: spread_copy(g, scale_rows[:, K_PASS * g : K_PASS * (g + 1)]),
            )
        task(
            "gd turn", "tensor", TENSOR_RUN, -1, ["gain columns"],
            lambda: spread_turn("gd", gd_cols), ("turned", "gd rows"),
        )
        task("gd rows", "scalar", 512, -1, ["gd turn"], lambda: spread_copy("gd", gd_rows[:]))

        max_256 = hold_each("max_256_", B, [PACK, ND // 2], BF16)
        max_128 = hold_each("max_128_", B, [PACK, ND // 4], BF16)
        row_max = hold_each("row_max", B, [PACK], F32)
        minus_max = hold_each("minus_max", B, [PACK], F32)
        exp_sum = hold_each("exp_sum", B, [PACK], F32)
        inverse = hold_each("inverse", B, [PACK], F32)
        exps = hold_each("exps", B, [PACK, ND], F32)
        d_rows = hold_each("d_rows", B, [PACK, ND], BF16)
        d_packed = hold_each("d_packed", B, [PACK, P, PACK], BF16)
        d_codes = hold_each("d_codes", B, [W], U32)
        d_scales = hold_each("d_scales", B, [W], U8)
        turned = {}

        def max_to_256(b, half):
            ts = slice(2 * half, 2 * half + 2)
            nc.vector.tensor_max(
                out=max_256[b][:, ts, :], in0=dl_raw[b][:, ts, 0 : ND // 2], in1=dl_raw[b][:, ts, ND // 2 :]
            )

        def max_to_128(b):
            nc.vector.tensor_max(out=max_128[b][:], in0=max_256[b][:, :, 0 : ND // 4], in1=max_256[b][:, :, ND // 4 :])

        def max_to_1(b):
            nc.vector.reduce_max(out=row_max[b][:], in_=max_128[b][:], axis=mybir.AxisListType.X)

        def negate_max(b):
            nc.vector.tensor_scalar(out=minus_max[b][:], in0=row_max[b][:], scalar1=-1.0, scalar2=None, op0=ALU.mult)

        def exponentials(b, t):
            nc.scalar.activation(
                out=exps[b][:, t, :], in_=dl_raw[b][:, t, :], func=ACT.Exp,
                bias=minus_max[b][:, t : t + 1], accum_out=exp_sum[b][:, t : t + 1],
            )

        def invert(b):
            nc.vector.reciprocal(out=inverse[b][:], in_=exp_sum[b][:])

        def depth(b, t):
            nc.vector.scalar_tensor_tensor(
                out=d_rows[b][:, t, :], in0=exps[b][:, t, :], scalar=inverse[b][:, t : t + 1], in1=gd_rows[:],
                op0=ALU.mult, op1=ALU.mult,
            )

        def turn_two(key, words_of):
            bank = psum_turned.tile([P, 2, 2, P], F32, name="bank")
            for j in range(2):
                turn_words(words_of(j), bank[:, j])
            turned[key] = bank

        def pack_two(key, dst):
            nc.scalar.copy(
                out=as_words(dst, "p j n k -> p (j n k)").rearrange("p (j n u) -> p j n u", j=2, u=2),
                in_=turned[key][:].rearrange("p j u n -> p j n u"),
            )

        def turn_depth(b, half):
            turn_two(
                ("d", b, half),
                lambda j: as_words(d_rows[b][:, 2 * half + j : 2 * half + j + 1, :], "p t n -> p (t n)"),
            )

        def quantise_depth(b):
            nc.vector.quantize_mx(
                out=d_codes[b][:].bitcast(FP8X4), scales=d_scales[b][:],
                in_=d_packed[b][:].rearrange("p t w k -> p (t w k)"),
            )

        for b in range(B):
            due = DUE["depth"][b]
            for half in range(2):
                task(("max 256", b, half), "vector", 256, b - 8, [("dl", b, half)], lambda b=b, half=half: max_to_256(b, half))
            task(("max 128", b), "vector", 256, b - 7, [("max 256", b, 0), ("max 256", b, 1)], lambda b=b: max_to_128(b))
            task(("max 1", b), "vector", 512, b - 6, [("max 128", b)], lambda b=b: max_to_1(b))
            task(("minus max", b), "vector", 10, b - 5, [("max 1", b)], lambda b=b: negate_max(b))
            for t in range(PACK):
                task(("exp", b, t), "scalar", 560, DUE["exp"][b], [("minus max", b)], lambda b=b, t=t: exponentials(b, t))
            task(("inverse", b), "vector", 40, due, [("exp", b, t) for t in range(PACK)], lambda b=b: invert(b))
            for t in range(PACK):
                task(
                    ("depth", b, t), "vector", 512, due + DUE["depth step"] * t, [("inverse", b), "gd rows"],
                    lambda b=b, t=t: depth(b, t),
                )
            for half in range(2):
                task(
                    ("d turn", b, half), "tensor", TENSOR_RUN, due, [("depth", b, 2 * half), ("depth", b, 2 * half + 1)],
                    lambda b=b, half=half: turn_depth(b, half), ("turned", ("d packed", b, half)),
                )
                task(
                    ("d packed", b, half), "scalar", 512, due, [("d turn", b, half)],
                    lambda b=b, half=half: pack_two(("d", b, half), d_packed[b][:, 2 * half : 2 * half + 2, :, :]),
                )
            task(("d codes", b), "vector", 512, due + 2, [("d packed", b, 0), ("d packed", b, 1)], lambda b=b: quantise_depth(b))

        ray_packed = hold("ray_packed", [CHUNKS, P, PACK], BF16)
        tm_packed = [hold("tm_packed", [CHUNKS, P, PACK], BF16)] * B
        tm_codes = hold_each("tm_codes", B, [CELLS], U32)
        tm_scales = hold_each("tm_scales", B, [CELLS], U8)
        rd = {}

        def turn_ray(i):
            turn_two(("ray", i), lambda j: as_words(ray_raw[:, 2 * i + j : 2 * i + j + 1, :], "p c w -> p (c w)"))

        def transport(b, c):
            bank = psum_sums.tile([P, PACK, P], F32, name="sums")
            for t in range(PACK):
                nc.tensor.matmul_mx(
                    out=bank[:, t, :],
                    lhsT=d_codes[b][:, P * t : P * (t + 1)].bitcast(FP8X4),
                    lhsT_scale=d_scales[b][:, P * t : P * (t + 1)],
                    rhs=ring[:, 2 * P * c : 2 * P * (c + 1)].bitcast(FP4X4),
                    rhs_scale=w_scales[:, G * O + P * c : G * O + P * (c + 1)],
                    start=True,
                    stop=True,
                )
            rd[b, c] = bank

        def weigh(b, c):
            nc.vector.tensor_tensor(
                out=tm_packed[b][:, c, :, :], in0=rd[b, c][:].rearrange("p t n -> p n t"), in1=ray_packed[:, c, :, :],
                op=ALU.mult,
            )

        def quantise_transport(b, c):
            nc.vector.quantize_mx(
                out=tm_codes[b][:, P * c : P * (c + 2)].bitcast(FP8X4),
                scales=tm_scales[b][:, P * c : P * (c + 2)],
                in_=tm_packed[b][:, c : c + 2, :, :].rearrange("p c n k -> p (c n k)"),
            )

        for i in range(CHUNKS // 2):
            due = DUE["ray"] + DUE["ray step"] * i
            task(
                ("ray turn", i), "tensor", TENSOR_RUN, due, ["ray"], lambda i=i: turn_ray(i),
                ("turned", ("ray packed", i)),
            )
            task(
                ("ray packed", i), "scalar", 512, due, [("ray turn", i)],
                lambda i=i: pack_two(("ray", i), ray_packed[:, 2 * i : 2 * i + 2, :, :]),
            )
        for b in range(B):
            for c in range(CHUNKS):
                due = DUE["transport"][b] + DUE["transport step"][b] * c
                if b == 0 and c >= LATE_CHUNK:
                    due = DUE["late transport"] + c
                task(
                    ("rd", b, c), "tensor", TENSOR_RUN // 2, due - 1, [("d codes", b), "ring"],
                    lambda b=b, c=c: transport(b, c), ("sums", ("tm", b, c)),
                )
                after = [("rd", b, c), ("ray packed", c // 2)]
                if b:
                    after = after + [("tm codes", b - 1, c // 2)]
                task(("tm", b, c), "vector", 512, due, after, lambda b=b, c=c: weigh(b, c))
                if c % 2 == 1:
                    task(
                        ("tm codes", b, c // 2), "vector", 256, due + DUE["transport codes"],
                        [("tm", b, c - 1), ("tm", b, c)], lambda b=b, c=c: quantise_transport(b, c - 1),
                    )

        m = hold_each("m", B, [PACK, O], F32)
        m_sum = hold_each("m_sum", B, [PACK], F32)
        offset = hold_each("offset", B, [PACK], F32)
        ctx_halves = [hold("ctx_halves", [2, O, 2], BF16)] * B
        ctx_packed = [hold("ctx_packed", [O, PACK], BF16)] * B
        ctx_codes = hold_each("ctx_codes", B, [O], U32)
        ctx_scales = hold_each("ctx_scales", B, [O], U8)
        x_rows, x_packed, x_codes, x_scales, x_halves, y, result_bank = {}, {}, {}, {}, {}, {}, {}

        def pair_tiles(s):
            x_packed[s] = flow.tile([P, G, 2, P, PACK], BF16, name="x_packed_s", align_bytes=64, bufs=SLOTS["pairs"])
            x_codes[s] = flow.tile([P, G, 2, P], U32, name="x_codes_s", align_bytes=64, bufs=SLOTS["codes"])
            x_scales[s] = flow.tile([P, G, 2, P], U8, name="x_scales_s", align_bytes=64, bufs=SLOTS["codes"])

        def scale_unit(q):
            if q % 2 == 0:
                pair_tiles(q // 2)
            x_rows[q] = flow.tile([P, C], BF16, name="x_rows_q", align_bytes=64, bufs=SLOTS["rows"])
            nc.vector.tensor_tensor(
                out=x_rows[q][:], in0=x_raw[q // PACK][:, q % PACK, :].bitcast(F8), in1=scale_rows[:], op=ALU.mult
            )

        def turn_unit(q):
            turn_two(("x", q), lambda g: x_rows[q][:, K_PASS * g : K_PASS * (g + 1)].bitcast(F32))

        def pack_unit(q):
            s, k = divmod(q, 2)
            words = as_words(x_packed[s][:], "p g k r t -> p (g k r t)").rearrange("p (g k r u) -> p g k r u", g=G, k=2, u=2)
            nc.scalar.copy(out=words[:, :, k], in_=turned["x", q][:].rearrange("p g u r -> p g r u"))

        def widen_unit(q):
            x_rows[q] = flow.tile([P, C], BF16, name="x_wide_q", align_bytes=64, bufs=SLOTS["wide"])
            nc.scalar.copy(out=x_rows[q][:], in_=x_raw[q // PACK][:, q % PACK, :].bitcast(F8))

        def turn_pair(s, g):
            if g == 0:
                x_halves[s] = flow.tile([P, G, 2, 2 * P, 2], BF16, name="x_halves_s", align_bytes=64, bufs=SLOTS["halves"])
            turn_two(("pair", s, g), lambda k: x_rows[2 * s + k][:, K_PASS * g : K_PASS * (g + 1)].bitcast(F32))

        def scale_turned(s, g, u):
            bank = turned["pair", s, g][:].rearrange("p k u r -> p (k u r)").bitcast(BF16)
            values = bank.rearrange("p (k u r e) -> p k u r e", k=2, u=2, e=2)
            for e in range(2):
                nc.scalar.activation(
                    out=x_halves[s][:, g, u, :, e].rearrange("p (k r) -> p k r", k=2),
                    in_=values[:, :, u, :, e],
                    func=ACT.Copy,
                    scale=scales[:, g, 2 * u + e : 2 * u + e + 1],
                )

        def weave_pair(s):
            pair_tiles(s)
            copy = nc.scalar.copy if s in SCALAR_WEAVES else nc.vector.tensor_copy
            copy(
                out=as_words(x_packed[s][:], "p g k r t -> p (g k r t)").rearrange("p (g c u) -> p g c u", g=G, u=2),
                in_=as_words(x_halves[s][:], "p g u c e -> p (g u c e)").rearrange("p (g u c) -> p g c u", g=G, u=2),
            )

        def quantise_pair(s):
            nc.vector.quantize_mx(
                out=x_codes[s][:].rearrange("p g k r -> p (g k r)").bitcast(FP8X4),
                scales=x_scales[s][:].rearrange("p g k r -> p (g k r)"),
                in_=x_packed[s][:].rearrange("p g k r t -> p (g k r t)"),
            )

        def project(q):
            s, k = divmod(q, 2)
            y[q] = psum_sums.tile([P, O], F32, name="sums")
            for g in range(G):
                nc.tensor.matmul_mx(
                    out=y[q][:],
                    lhsT=x_codes[s][:, g, k, :].bitcast(FP8X4),
                    lhsT_scale=x_scales[s][:, g, k, :],
                    rhs=wc[:, g, :].bitcast(FP4X4),
                    rhs_scale=w_scales[:, O * g : O * (g + 1)],
                    start=(g == 0),
                    stop=(g == G - 1),
                )

        def height_max(q):
            i, t = divmod(q, PACK)
            b, h = divmod(i, HI)
            running = m[b][:, t, :]
            if h == 0:
                nc.scalar.copy(out=running, in_=y[q][:])
            elif h < HI - 1:
                nc.vector.tensor_max(out=running, in0=y[q][:], in1=running)
            else:
                nc.vector.scalar_tensor_tensor(
                    out=running, in0=y[q][:], scalar=1.0, in1=running, op0=ALU.mult, op1=ALU.max,
                    accum_out=m_sum[b][:, t : t + 1],
                )

        def centring_offset(b, t):
            nc.gpsimd.tensor_scalar(
                out=offset[b][:, t : t + 1], in0=m_sum[b][:, t : t + 1], scalar1=gw_mean[:, t : t + 1], scalar2=None,
                op0=ALU.mult,
            )

        def centre(b, t):
            nc.scalar.activation(
                out=ctx_halves[b][:, t // 2, :, t % 2], in_=m[b][:, t, :], func=ACT.Identity,
                scale=gw_cols[:, t : t + 1], bias=offset[b][:, t : t + 1],
            )

        def weave_context(b):
            copy = nc.scalar.copy if b in SCALAR_CTX_WEAVES else nc.vector.tensor_copy
            copy(
                out=as_words(ctx_packed[b][:], "p o t -> p (o t)").rearrange("p (o u) -> p o u", u=2),
                in_=as_words(ctx_halves[b][:], "p u o e -> p (u o e)").rearrange("p (u o) -> p o u", u=2),
            )

        def quantise_context(b):
            nc.vector.quantize_mx(
                out=ctx_codes[b][:].bitcast(FP8X4), scales=ctx_scales[b][:],
                in_=ctx_packed[b][:].rearrange("p o t -> p (o t)"),
            )

        def result(b, c):
            bank = psum_sums.tile([P, O], F32, name="sums")
            nc.tensor.matmul_mx(
                out=bank[:],
                lhsT=tm_codes[b][:, P * c : P * (c + 1)].bitcast(FP8X4),
                lhsT_scale=tm_scales[b][:, P * c : P * (c + 1)],
                rhs=ctx_codes[b][:].bitcast(FP8X4),
                rhs_scale=ctx_scales[b][:],
                start=True,
                stop=True,
            )
            result_bank[b, c] = bank

        def store(b, c, engine):
            rows = stores.tile([P, O], F32, name="rows", align_bytes=64)
            copy = nc.vector.tensor_copy if engine == "vector" else nc.scalar.copy
            copy(out=rows[:], in_=result_bank[b, c][:])
            nc.sync.dma_start(out=out[b, P * c : P * (c + 1), :], in_=rows[:])

        for s in range(N_UNITS // 2):
            pair = (2 * s, 2 * s + 1)
            pair_holds = [("pairs", ("x codes", s)), ("codes", ("y", 2 * s + 1))]
            if s in SCALAR_PAIRS:
                for q in pair:
                    task(
                        ("x rows", q), "scalar", 1024, q + DUE["widen"], [("x", q // PACK, q % PACK)],
                        lambda q=q: widen_unit(q), ("wide", ("pair turn", s, 1)),
                    )
                for g in range(G):
                    due = 2 * s + DUE["pair turn"] + 2 * g
                    after = [("x rows", q) for q in pair]
                    if g:
                        after = after + [("pair turn", s, 0)]
                    task(
                        ("pair turn", s, g), "tensor", TENSOR_RUN, due, after, lambda s=s, g=g: turn_pair(s, g),
                        ("turned", ("x halves", s, g, 1)), *([] if g else [("halves", ("weave", s))]),
                    )
                    for u in range(2):
                        task(
                            ("x halves", s, g, u), "scalar", 780, due + u, [("pair turn", s, g)],
                            lambda s=s, g=g, u=u: scale_turned(s, g, u),
                        )
                task(
                    ("weave", s), "scalar" if s in SCALAR_WEAVES else "vector", 1024 if s in SCALAR_WEAVES else 512, 2 * s,
                    [("x halves", s, g, u) for g in range(G) for u in range(2)], lambda s=s: weave_pair(s), *pair_holds,
                )
                packed = [("weave", s)]
            else:
                for q in pair:
                    first_unit = [("x rows", q - 1)] if q % 2 else []
                    task(
                        ("x rows", q), "vector", 1024, q,
                        [("x", q // PACK, q % PACK), ("scale rows", 0), ("scale rows", 1)] + first_unit,
                        lambda q=q: scale_unit(q), ("rows", ("x turn", q)), *([] if q % 2 else pair_holds),
                    )
                    task(
                        ("x turn", q), "tensor", TENSOR_RUN, q, [("x rows", q)], lambda q=q: turn_unit(q),
                        ("turned", ("x packed", q)),
                    )
                    task(("x packed", q), "scalar", 512, q, [("x turn", q)], lambda q=q: pack_unit(q))
                packed = [("x packed", q) for q in pair]
            task(("x codes", s), "vector", 512, 2 * s + DUE["quantise"], packed, lambda s=s: quantise_pair(s))
            for q in pair:
                h = q // PACK % HI
                first_unit = [("y", q - 1)] if q % 2 else []
                task(
                    ("y", q), "tensor", TENSOR_RUN, q + DUE["project"], [("x codes", s), "wc"] + first_unit,
                    lambda q=q: project(q), ("sums", ("m", q)),
                )
                before = [("m", q - PACK)] if h else []
                task(
                    ("m", q), "vector" if h else "scalar", 512, q + DUE["height maximum"], [("y", q)] + before,
                    lambda q=q: height_max(q),
                )
        for b in range(B):
            halves_free = [("ctx weave", b - 1)] if b else []
            packed_free = [("ctx codes", b - 1)] if b else []
            for t in range(PACK):
                task(
                    ("offset", b, t), "gpsimd", 200, 0, [("m", (b * HI + HI - 1) * PACK + t), "gain columns"],
                    lambda b=b, t=t: centring_offset(b, t),
                )
                task(
                    ("ctx halves", b, t), "scalar", 780, DUE["centre"] + DUE["centre step"] * b,
                    [("offset", b, t)] + halves_free, lambda b=b, t=t: centre(b, t),
                )
            due = DUE["context"] + DUE["context step"] * b
            on_scalar = b in SCALAR_CTX_WEAVES
            task(
                ("ctx weave", b), "scalar" if on_scalar else "vector", 1024 if on_scalar else 512, due,
                [("ctx halves", b, t) for t in range(PACK)] + packed_free, lambda b=b: weave_context(b),
            )
            task(("ctx codes", b), "vector", 512, due, [("ctx weave", b)], lambda b=b: quantise_context(b))
            for c in range(CHUNKS):
                engine = "vector" if b == B - 1 and c in VECTOR_RESULTS else "scalar"
                due = DUE["result"] + DUE["result step"] * c + DUE["result batch step"] * b
                task(
                    ("result", b, c), "tensor", TENSOR_RUN // 2, due, [("ctx codes", b), ("tm codes", b, c // 2)],
                    lambda b=b, c=c: result(b, c), ("sums", ("store", b, c)),
                )
                task(
                    ("store", b, c), engine, 512, due, [("result", b, c)],
                    lambda b=b, c=c, engine=engine: store(b, c, engine),
                )

        for call in list_order(tasks, arrived):
            call()
